import numpy as np
import ml_dtypes


def mxq(x, axis, fmt="e4m3"):
    dtype, down = {"e4m3": (ml_dtypes.float8_e4m3fn, 7), "e5m2": (ml_dtypes.float8_e5m2, 14)}[fmt]
    v = np.moveaxis(np.asarray(x, np.float32).astype(ml_dtypes.bfloat16).astype(np.float64), axis, -1)
    blocks = v.reshape(v.shape[:-1] + (-1, 32))
    amax = np.abs(blocks).max(-1, keepdims=True)
    byte = np.maximum(np.where(amax > 0, np.frexp(amax)[1] - 1 + 127, 0) - down, 1)
    scale = np.exp2(byte - 127.0)
    codes = (blocks / scale).astype(np.float32).astype(dtype).astype(np.float64)
    return np.moveaxis((codes * scale).reshape(v.shape), -1, axis)


WIDE = False


def mx_kscale(k):
    if not WIDE:
        return np.ones(k)
    levels = np.array([10, -10, 5, -5, 0])
    if k % 512:
        return np.exp2(np.random.permutation(np.resize(levels, k // 32))).repeat(32)
    a = np.empty((k // 512, 16))
    for p in range(k // 512):
        a[p, :8] = np.random.permutation(np.resize(levels, 8))
        for g in range(8):
            far = levels[np.abs(levels - a[p, g]) >= 10]
            a[p, g + 8] = far[np.random.randint(len(far))]
    return np.exp2(a.ravel()).repeat(32)


def f64(x):
    return np.asarray(x).astype(np.float64)


def striped(idx):
    return np.tile(idx.reshape(-1, 16).T, (8, 1)).astype(np.uint16)


def unstriped(offs):
    return offs[:16].T.reshape(-1).astype(np.int64)


E2M1 = np.array([0.0, 0.5, 1.0, 1.5, 2.0, 3.0, 4.0, 6.0, -0.0, -0.5, -1.0, -1.5, -2.0, -3.0, -4.0, -6.0])


def pack_weight(w, fmt):
    k, n = w.shape
    w = f64(np.asarray(w, np.float32).astype(ml_dtypes.bfloat16)).reshape(k // 32, 32, n)
    amax = np.abs(w).max(1)
    if fmt == "e4m3":
        byte = np.frexp(amax)[1] - 1 + 127 - 7
    else:
        mant, ex = np.frexp(amax / 6.0)
        byte = np.where(mant > 0.5, ex, ex - 1) + 127
    byte = np.clip(np.where(amax > 0, byte, 1), 1, 254)
    scaled = (w * np.exp2(127.0 - byte)[:, None, :]).reshape(k, n).astype(np.float32)
    by_word = np.ascontiguousarray(scaled.reshape(k // 512, 128, 4, n).transpose(0, 1, 3, 2))
    if fmt == "e4m3":
        words = by_word.astype(ml_dtypes.float8_e4m3fn).view(np.uint8)
    else:
        c = by_word.astype(ml_dtypes.float4_e2m1fn).view(np.uint8) & 0xF
        words = (c[..., 0::2] | (c[..., 1::2] << 4)).reshape(k // 512, 128, 2 * n)
    return np.ascontiguousarray(words), np.ascontiguousarray(byte.astype(np.uint8).reshape(k // 512, 16, n))


def unpack_weight(words, scales, fmt):
    g, _, n = scales.shape
    words = np.ascontiguousarray(words).reshape(g, 128, n, -1)
    if fmt == "e4m3":
        vals = words.view(ml_dtypes.float8_e4m3fn).astype(np.float64)
    else:
        nib = np.empty((g, 128, n, 4), np.uint8)
        nib[..., 0::2] = words & 0xF
        nib[..., 1::2] = words >> 4
        vals = E2M1[nib]
    vals = vals * np.repeat(np.exp2(scales.astype(np.float64) - 127.0), 8, axis=1)[..., None]
    return vals.transpose(0, 1, 3, 2).reshape(g * 512, n)


def gelu(v):
    return 0.5 * v * (1.0 + np.tanh(np.sqrt(2.0 / np.pi) * (v + 0.044715 * v**3)))


def often(T, S):
    return np.random.permutation(T)[(T * np.random.uniform(0, 1, S) ** 4).astype(np.int64)]


K, M, H, N, R, T, S = 1024, 512, 1024, 512, 1536, 4096, 1024

def setup_inputs():
    n = np.random.standard_normal
    s = mx_kscale(K)[:, None]
    s2 = mx_kscale(M)[:, None]
    u = mx_kscale(H)[:, None]
    tab_words, tab_scales = pack_weight(n((K, T)) * s, "e4m3")
    tab2_words, tab2_scales = pack_weight(n((M, T)) * s2, "e2m1")
    w1 = n((K, R)) / np.sqrt(K) / s
    w1[:, :H] = w1[:, :H] * u.T
    w1_words, w1_scales = pack_weight(w1, "e2m1")
    w2 = (n((M, H)) / np.sqrt(M) / s2 * u.T).astype(np.float32)
    soft = (np.random.uniform(0.5, 1.5, H) * u[:, 0] ** 2).astype(np.float32)
    w3_words, w3_scales = pack_weight(n((H, N)) / np.sqrt(H) / u, "e4m3")
    return {"tab_words": tab_words, "tab_scales": tab_scales,
            "tab2_words": tab2_words, "tab2_scales": tab2_scales,
            "offs": striped(often(T, S)), "offs2": striped(often(T, S)),
            "w1_words": w1_words, "w1_scales": w1_scales, "w2": w2, "soft": soft,
            "w3_words": w3_words, "w3_scales": w3_scales}

def reference(tab_words, tab_scales, tab2_words, tab2_scales, offs, offs2,
              w1_words, w1_scales, w2, soft, w3_words, w3_scales):
    v = unpack_weight(tab_words, tab_scales, "e4m3")[:, unstriped(offs)]
    v2 = unpack_weight(tab2_words, tab2_scales, "e2m1")[:, unstriped(offs2)]
    w1 = unpack_weight(w1_words, w1_scales, "e2m1")
    w3 = unpack_weight(w3_words, w3_scales, "e4m3")
    a = w1.T @ v
    b = mxq(f64(w2), 0, "e4m3").T @ v2
    sq = np.square(np.concatenate([a[:H], b], axis=0))
    h = np.sqrt(sq[:H] + sq[H:] + f64(soft)[:, None])
    y = w3.T @ mxq(h, 0, "e4m3")
    return y * (1.0 / (1.0 + np.exp(-a[H:])))

@@ -1,0 +1,299 @@
+from contextlib import ExitStack
+
+import concourse.mybir as mybir
+
+K, M, H, N, R, T, S = 1024, 512, 1024, 512, 1536, 4096, 1024
+FLOPS = 2 * S * (K * R + M * H + H * N)
+
+F32 = mybir.dt.float32
+BF16 = mybir.dt.bfloat16
+I32 = mybir.dt.int32
+U32 = mybir.dt.uint32
+U16 = mybir.dt.uint16
+U8 = mybir.dt.uint8
+FP8X4 = mybir.dt.float8_e4m3fn_x4
+FP4X4 = mybir.dt.float4_e2m1fn_x4
+ACT = mybir.ActivationFunctionType
+ALU = mybir.AluOpType
+
+P = 128
+PACK = 4
+PASS = P * PACK
+BANK = 512
+HALVES = S // BANK
+TAIL = 256
+
+
+def tile_list_row_servoing_kernel(
+    tc, tab_words, tab_scales, tab2_words, tab2_scales, offs, offs2,
+    w1_words, w1_scales, w2, soft, w3_words, w3_scales, out,
+):
+    nc = tc.nc
+    k_passes = K // PASS
+    h_passes = H // PASS
+    n_tiles = N // P
+    list_cols = BANK // 16
+
+    with ExitStack() as ctx:
+        keep = ctx.enter_context(tc.tile_pool(name="keep", bufs=1))
+        ring = ctx.enter_context(tc.tile_pool(name="ring", bufs=2))
+        psum = ctx.enter_context(tc.psum_pool(name="psum", bufs=8))
+
+        def held(name, shape, dtype, tag=""):
+            return keep.tile(shape, dtype, name=name, tag=tag or name, align_bytes=64)
+
+        idx = held("idx", [P, S // 16], U16)
+        idx2 = held("idx2", [P, S // 16], U16)
+        tab_win = [held("tab_win%d" % a, [P, T], I32) for a in range(k_passes)]
+        tab2_win = held("tab2_win", [P, T], U16)
+        tab_scale_win = held("tab_scale_win", [P, T], U8)
+        tab2_scale_win = held("tab2_scale_win", [P, T], U8)
+        w2_raw = [held("w2_raw%d" % b, [P, PACK, PASS], F32) for b in range(h_passes)]
+        w1_err_raw = held("w1_err_raw", [P, k_passes, H], U16)
+        w1_gate = held("w1_gate", [P, k_passes, 2 * N], U8)
+        w1_scale_raw = held("w1_scale_raw", [P, k_passes, R], U8)
+        soft_sb = held("soft_sb", [P, h_passes, PACK], F32)
+        v_plane_moved = held("v_plane_moved", [P, S], U8)
+        warm = held("warm", [P, 1], F32)
+        warm_out = held("warm_out", [P, 1], F32)
+
+        nc.gpsimd.memset(warm[:], 0.0)
+        nc.scalar.activation(warm_out[:], warm[:], ACT.Sigmoid)
+        for plane in (tab2_scale_win, tab_scale_win, w1_scale_raw, v_plane_moved):
+            nc.vector.memset(plane[:].bitcast(I32), 0)
+
+        w2_rows = w2.rearrange("(p j) r -> p j r", j=PACK)
+        w1_rows = w1_words.rearrange("a p c -> p a c")
+        nc.sync.dma_start(idx2[:], offs2)
+        nc.sync.dma_start(idx[:], offs)
+        nc.sync.dma_start(soft_sb[:], soft.rearrange("(b p t) -> p b t", p=P, t=PACK))
+        for c in range(2):
+            for j in range(0, PACK, 2):
+                cols = slice(c * PASS // 2, (c + 1) * PASS // 2)
+                nc.sync.dma_start(w2_raw[0][:, j : j + 2, cols], w2_rows[:, j : j + 2, cols])
+        nc.sync.dma_start(w1_gate[:].bitcast(I32), w1_rows[:, :, 2 * H : 2 * R].bitcast(I32))
+        for r in range(4):
+            nc.sync.dma_start(tab2_scale_win[r:P:32, :].bitcast(I32), tab2_scales[0, r:16:4, :].bitcast(I32))
+        nc.sync.dma_start(tab2_win[:].bitcast(I32), tab2_words[0].bitcast(I32))
+        for q in (0, 2, 1, 3):
+            nc.sync.dma_start(
+                tab_scale_win[32 * q : 32 * q + 8, :].bitcast(I32),
+                tab_scales[:, 4 * q : 4 * q + 4, :].bitcast(I32),
+            )
+        nc.sync.dma_start(w2_raw[1][:], w2_rows[:, :, PASS : 2 * PASS])
+        nc.sync.dma_start(w1_err_raw[:].bitcast(I32), w1_rows[:, :, 0 : 2 * H].bitcast(I32))
+        for r in range(4):
+            nc.sync.dma_start(
+                w1_scale_raw[r:P:32, :, :].bitcast(I32),
+                w1_scales[:, r:16:4, :].rearrange("a q c -> q a c").bitcast(I32),
+            )
+        for a in range(k_passes):
+            nc.sync.dma_start(tab_win[a][:], tab_words[a].rearrange("p t i -> p (t i)").bitcast(I32))
+
+        v2_plane = held("v2_plane", [P, S], U8)
+        nc.vector.tensor_copy(v2_plane[:], tab2_scale_win[:].indirect(idx2[:]))
+
+        w2_codes = []
+        w2_plane = []
+
+        def quantise_w2(b, copiers):
+            grouped = held("w2_grouped%d" % b, [P, PACK, P, PACK], BF16)
+            src = w2_raw[b][:].rearrange("p j (m t) -> p m j t", t=PACK)
+            dst = grouped[:].rearrange("p t m j -> p m j t")
+            for c, copier in enumerate(copiers):
+                rows = slice(c * P // 2, (c + 1) * P // 2)
+                copier(dst[:, rows], src[:, rows])
+            codes = held("w2_codes%d" % b, [P, PASS], U32)
+            plane = held("w2_plane%d" % b, [P, PASS], U8)
+            nc.vector.quantize_mx(
+                out=codes[:].bitcast(FP8X4), scales=plane[:],
+                in_=grouped[:].rearrange("p t m j -> p (t m j)"),
+            )
+            w2_codes.append(codes)
+            w2_plane.append(plane)
+
+        quantise_w2(0, (nc.scalar.copy, nc.scalar.copy))
+
+        v2_codes = []
+        for hf in range(HALVES):
+            codes = held("v2_codes%d" % hf, [P, BANK], U16)
+            nc.vector.tensor_copy(codes[:], tab2_win[:].indirect(idx2[:, hf * list_cols : (hf + 1) * list_cols]))
+            v2_codes.append(codes)
+
+        v_scale_rows = held("v_scale_rows", [P, S], U8)
+        nc.vector.tensor_copy(v_scale_rows[:], tab_scale_win[:].indirect(idx[:]))
+        for r in range(4):
+            nc.scalar.dma_start(
+                v_plane_moved[r:P:32, :].bitcast(I32), v_scale_rows[4 + r : P : 32, :].bitcast(I32)
+            )
+        v_plane = [v_scale_rows, v_plane_moved]
+
+        quantise_w2(1, (nc.scalar.copy, nc.vector.tensor_copy))
+
+        w3_plane = held("w3_plane", [P, N], U8, tag="tab_scale_win")
+        w3_codes = held("w3_codes", [P, h_passes, N], I32, tag="w2_raw1")
+        nc.vector.memset(w3_plane[:].bitcast(I32), 0)
+        nc.sync.dma_start(w3_codes[:], w3_words.rearrange("a p c i -> p a (c i)").bitcast(I32))
+        for q in (0, 2, 1, 3):
+            nc.sync.dma_start(
+                w3_plane[32 * q : 32 * q + 8, :].bitcast(I32),
+                w3_scales[:, 4 * q : 4 * q + 4, :].bitcast(I32),
+            )
+
+
+        b_sq = {}
+        for b in range(h_passes):
+            for hf in range(HALVES):
+                cols = slice(hf * BANK, (hf + 1) * BANK)
+                for t in range(PACK):
+                    bank = psum.tile([P, BANK], F32, name="bank")
+                    nc.tensor.matmul_mx(
+                        out=bank[:],
+                        lhsT=w2_codes[b][:, t * P : (t + 1) * P].bitcast(FP8X4),
+                        lhsT_scale=w2_plane[b][:, t * P : (t + 1) * P],
+                        rhs=v2_codes[hf][:].bitcast(FP4X4),
+                        rhs_scale=v2_plane[:, cols],
+                        start=True, stop=True,
+                    )
+                    sq = held("b_sq%d%d%d" % (b, hf, t), [P, BANK], F32)
+                    nc.scalar.activation(sq[:], bank[:], ACT.Square)
+                    b_sq[(b, hf, t)] = sq
+
+        w1_err = []
+        w1_err_plane = []
+        for a in range(k_passes):
+            words = held("w1_err%d" % a, [P, H], U16)
+            nc.vector.tensor_copy(
+                words[:].rearrange("p (b t c i) -> p b c t i", b=h_passes, t=PACK, i=8),
+                w1_err_raw[:, a, :].rearrange("p (b c i t) -> p b c t i", b=h_passes, t=PACK, i=8),
+            )
+            plane = held("w1_err_plane%d" % a, [P, H], U8)
+            nc.vector.tensor_copy(
+                plane[:].rearrange("p (b t c i) -> p b c t i", b=h_passes, t=PACK, i=16),
+                w1_scale_raw[:, a, 0:H].rearrange("p (b c i t) -> p b c t i", b=h_passes, t=PACK, i=16),
+            )
+            w1_err.append(words)
+            w1_err_plane.append(plane)
+
+        v_codes = {}
+        for a in range(k_passes):
+            for hf in range(HALVES):
+                codes = held("v_codes%d%d" % (a, hf), [P, BANK], U32)
+                nc.vector.tensor_copy(
+                    codes[:],
+                    tab_win[a][:].bitcast(U32).indirect(idx[:, hf * list_cols : (hf + 1) * list_cols]),
+                )
+                v_codes[(a, hf)] = codes
+
+        def first_product(hf, codes_of, plane_of):
+            bank = psum.tile([P, BANK], F32, name="bank")
+            for a in range(k_passes):
+                nc.tensor.matmul_mx(
+                    out=bank[:],
+                    lhsT=codes_of(a).bitcast(FP4X4),
+                    lhsT_scale=plane_of(a),
+                    rhs=v_codes[(a, hf)][:].bitcast(FP8X4),
+                    rhs_scale=v_plane[a][:, hf * BANK : (hf + 1) * BANK],
+                    start=(a == 0), stop=(a == k_passes - 1),
+                )
+            return bank
+
+        gate = [held("gate%d" % hf, [P, n_tiles, BANK], F32) for hf in range(HALVES)]
+
+        def make_gate(hf, nt):
+            bank = first_product(
+                hf,
+                lambda a: w1_gate[:, a, 2 * P * nt : 2 * P * (nt + 1)],
+                lambda a: w1_scale_raw[:, a, H + P * nt : H + P * (nt + 1)],
+            )
+            nc.scalar.activation(gate[hf][:, nt, :], bank[:], ACT.Sigmoid)
+
+        def error_bank(hf, b, t):
+            cols = slice(b * PASS + t * P, b * PASS + (t + 1) * P)
+            return first_product(hf, lambda a: w1_err[a][:, cols], lambda a: w1_err_plane[a][:, cols])
+
+        def add_terms(total, a_sq, hf, b, t):
+            nc.vector.scalar_tensor_tensor(
+                total[:, t, :], a_sq, soft_sb[:, b, t : t + 1], b_sq[(b, hf, t)][:], ALU.add, ALU.add
+            )
+
+        def sum_on_scalar(hf, b):
+            total = ring.tile([P, PACK, BANK], F32, name="total", bufs=3, align_bytes=64)
+            for t in range(PACK):
+                bank = error_bank(hf, b, t)
+                a_sq = ring.tile([P, BANK], F32, name="a_sq", bufs=4, align_bytes=64)
+                nc.scalar.activation(a_sq[:], bank[:], ACT.Square)
+                add_terms(total, a_sq[:], hf, b, t)
+            return total
+
+        h_codes = {}
+        h_plane = {}
+
+        def magnitude(hf, b, total, c0, width):
+            h_grouped = ring.tile([P, width, PACK], BF16, name="h_grouped", bufs=3, align_bytes=64)
+            nc.scalar.activation(
+                h_grouped[:].rearrange("p (c i) t -> p c t i", i=4),
+                total[:, :, c0 : c0 + width].rearrange("p t (c i) -> p c t i", i=4),
+                ACT.Sqrt,
+            )
+            codes = held("h_codes%d%d_%d" % (hf, b, c0), [P, width], U32)
+            plane = held("h_plane%d%d_%d" % (hf, b, c0), [P, width], U8)
+            nc.vector.quantize_mx(
+                out=codes[:].bitcast(FP8X4), scales=plane[:],
+                in_=h_grouped[:].rearrange("p j t -> p (j t)"),
+            )
+            for c in range(c0, c0 + width, P):
+                h_codes[(hf, b, c)] = (codes, c - c0)
+                h_plane[(hf, b, c)] = plane
+
+        def steer(hf, c0, width):
+            per_bank = BANK // width
+            for n0 in range(0, n_tiles, per_bank):
+                bank = psum.tile([P, per_bank, width], F32, name="bank")
+                for i in range(per_bank):
+                    cols = slice((n0 + i) * P, (n0 + i + 1) * P)
+                    for b in range(h_passes):
+                        codes, at = h_codes[(hf, b, c0)]
+                        nc.tensor.matmul_mx(
+                            out=bank[:, i, :],
+                            lhsT=w3_codes[:, b, cols].bitcast(FP8X4),
+                            lhsT_scale=w3_plane[4 * b : P, cols],
+                            rhs=codes[:, at : at + width].bitcast(FP8X4),
+                            rhs_scale=h_plane[(hf, b, c0)][:, at : at + width],
+                            start=(b == 0), stop=(b == h_passes - 1),
+                        )
+                result = ring.tile([P, per_bank, width], F32, name="result", bufs=4, align_bytes=64)
+                nc.vector.tensor_tensor(
+                    result[:], bank[:], gate[hf][:, n0 : n0 + per_bank, c0 : c0 + width], ALU.mult
+                )
+                j0 = hf * BANK + c0
+                nc.sync.dma_start(
+                    out[n0 * P : (n0 + per_bank) * P, j0 : j0 + width].rearrange("(i p) j -> p i j", p=P),
+                    result[:],
+                )
+
+        for nt in range(n_tiles):
+            make_gate(0, nt)
+        total0 = ring.tile([P, PACK, BANK], F32, name="total", bufs=3, align_bytes=64)
+        a_plain = held("a_plain", [P, PACK, BANK], F32)
+        a_sq0 = held("a_sq0", [P, PACK, BANK], F32)
+        for t in range(PACK):
+            bank = error_bank(0, 0, t)
+            nc.vector.tensor_copy(a_plain[:, t, :], bank[:])
+            make_gate(1, t)
+            if t % 2 == 1:
+                pair = slice(t - 1, t + 1)
+                nc.vector.tensor_tensor(a_sq0[:, pair, :], a_plain[:, pair, :], a_plain[:, pair, :], ALU.mult)
+        for t in range(PACK):
+            add_terms(total0, a_sq0[:, t, :], 0, 0, t)
+
+        total1 = sum_on_scalar(0, 1)
+        magnitude(0, 0, total0, 0, BANK)
+        total2 = sum_on_scalar(1, 0)
+        magnitude(0, 1, total1, 0, BANK)
+        steer(0, 0, BANK)
+        total3 = sum_on_scalar(1, 1)
+        magnitude(1, 0, total2, 0, BANK)
+        for c0 in range(0, BANK, TAIL):
+            magnitude(1, 1, total3, c0, TAIL)
+            steer(1, c0, TAIL)

@@ -21,7 +21,8 @@ PACK = 4
 PASS = P * PACK
 BANK = 512
 HALVES = S // BANK
-TAIL = 256
+ON_VECTOR = (1, 3)
+TAIL = ((0, 256, 2), (256, 128, 4), (384, 128, 2))
 
 
 def tile_list_row_servoing_kernel(
@@ -39,8 +40,8 @@ def tile_list_row_servoing_kernel(
         ring = ctx.enter_context(tc.tile_pool(name="ring", bufs=2))
         psum = ctx.enter_context(tc.psum_pool(name="psum", bufs=8))
 
-        def held(name, shape, dtype, tag=""):
-            return keep.tile(shape, dtype, name=name, tag=tag or name, align_bytes=64)
+        def held(name, shape, dtype):
+            return keep.tile(shape, dtype, name=name, align_bytes=64)
 
         idx = held("idx", [P, S // 16], U16)
         idx2 = held("idx2", [P, S // 16], U16)
@@ -51,47 +52,47 @@ def tile_list_row_servoing_kernel(
         w2_raw = [held("w2_raw%d" % b, [P, PACK, PASS], F32) for b in range(h_passes)]
         w1_err_raw = held("w1_err_raw", [P, k_passes, H], U16)
         w1_gate = held("w1_gate", [P, k_passes, 2 * N], U8)
-        w1_scale_raw = held("w1_scale_raw", [P, k_passes, R], U8)
+        w1_scale_raw = held("w1_scale_raw", [P, R], U8)
+        w1_plane = [held("w1_plane%d" % a, [P, R], U8) for a in range(k_passes)]
+        w3_plane = held("w3_plane", [P, N], U8)
+        w3_codes = held("w3_codes", [P, h_passes, N], I32)
         soft_sb = held("soft_sb", [P, h_passes, PACK], F32)
-        v_plane_moved = held("v_plane_moved", [P, S], U8)
+        v_plane = [held("v_plane%d" % a, [P, S], U8) for a in range(k_passes)]
+        v2_plane = held("v2_plane", [P, S], U8)
         warm = held("warm", [P, 1], F32)
         warm_out = held("warm_out", [P, 1], F32)
 
         nc.gpsimd.memset(warm[:], 0.0)
         nc.scalar.activation(warm_out[:], warm[:], ACT.Sigmoid)
-        for plane in (tab2_scale_win, tab_scale_win, w1_scale_raw, v_plane_moved):
+        for plane in (tab2_scale_win, tab_scale_win, w1_scale_raw, v2_plane, *v_plane, w1_plane[1], w3_plane):
             nc.vector.memset(plane[:].bitcast(I32), 0)
+
+        def load_two_pass_scales(plane, scales):
+            for q in (0, 2, 1, 3):
+                nc.sync.dma_start(
+                    plane[32 * q : 32 * q + 8, :].bitcast(I32), scales[:, 4 * q : 4 * q + 4, :].bitcast(I32)
+                )
 
         w2_rows = w2.rearrange("(p j) r -> p j r", j=PACK)
         w1_rows = w1_words.rearrange("a p c -> p a c")
+        nc.sync.dma_start(w2_raw[0][:, :, 0 : PASS // 2], w2_rows[:, :, 0 : PASS // 2])
         nc.sync.dma_start(idx2[:], offs2)
+        nc.sync.dma_start(tab2_scale_win[4:P:8, :].bitcast(I32), tab2_scales[0].bitcast(I32))
+        nc.sync.dma_start(w2_raw[0][:, :, PASS // 2 : PASS], w2_rows[:, :, PASS // 2 : PASS])
         nc.sync.dma_start(idx[:], offs)
-        nc.sync.dma_start(soft_sb[:], soft.rearrange("(b p t) -> p b t", p=P, t=PACK))
-        for c in range(2):
-            for j in range(0, PACK, 2):
-                cols = slice(c * PASS // 2, (c + 1) * PASS // 2)
-                nc.sync.dma_start(w2_raw[0][:, j : j + 2, cols], w2_rows[:, j : j + 2, cols])
-        nc.sync.dma_start(w1_gate[:].bitcast(I32), w1_rows[:, :, 2 * H : 2 * R].bitcast(I32))
-        for r in range(4):
-            nc.sync.dma_start(tab2_scale_win[r:P:32, :].bitcast(I32), tab2_scales[0, r:16:4, :].bitcast(I32))
-        nc.sync.dma_start(tab2_win[:].bitcast(I32), tab2_words[0].bitcast(I32))
-        for q in (0, 2, 1, 3):
-            nc.sync.dma_start(
-                tab_scale_win[32 * q : 32 * q + 8, :].bitcast(I32),
-                tab_scales[:, 4 * q : 4 * q + 4, :].bitcast(I32),
-            )
-        nc.sync.dma_start(w2_raw[1][:], w2_rows[:, :, PASS : 2 * PASS])
-        nc.sync.dma_start(w1_err_raw[:].bitcast(I32), w1_rows[:, :, 0 : 2 * H].bitcast(I32))
-        for r in range(4):
-            nc.sync.dma_start(
-                w1_scale_raw[r:P:32, :, :].bitcast(I32),
-                w1_scales[:, r:16:4, :].rearrange("a q c -> q a c").bitcast(I32),
-            )
         for a in range(k_passes):
-            nc.sync.dma_start(tab_win[a][:], tab_words[a].rearrange("p t i -> p (t i)").bitcast(I32))
+            nc.sync.dma_start(tab_scale_win[4 + a : P : 8, :].bitcast(I32), tab_scales[a].bitcast(I32))
+        nc.sync.dma_start(tab2_win[:].bitcast(I32), tab2_words[0].bitcast(I32))
+        load_two_pass_scales(w1_scale_raw, w1_scales)
+        nc.sync.dma_start(w2_raw[1][:], w2_rows[:, :, PASS : 2 * PASS])
 
-        v2_plane = held("v2_plane", [P, S], U8)
-        nc.vector.tensor_copy(v2_plane[:], tab2_scale_win[:].indirect(idx2[:]))
+        v2_scale_rows = held("v2_scale_rows", [P, S], U8)
+        nc.vector.tensor_copy(v2_scale_rows[:], tab2_scale_win[:].indirect(idx2[:]))
+        for r in range(4):
+            nc.sync.dma_start(v2_plane[r:P:32, :].bitcast(I32), v2_scale_rows[8 * r + 4 : P : 32, :].bitcast(I32))
+
+        nc.sync.dma_start(w1_gate[:].bitcast(I32), w1_rows[:, :, 2 * H : 2 * R].bitcast(I32))
+        nc.sync.dma_start(tab_win[0][:], tab_words[0].rearrange("p t i -> p (t i)").bitcast(I32))
 
         w2_codes = []
         w2_plane = []
@@ -101,7 +102,7 @@ def tile_list_row_servoing_kernel(
             src = w2_raw[b][:].rearrange("p j (m t) -> p m j t", t=PACK)
             dst = grouped[:].rearrange("p t m j -> p m j t")
             for c, copier in enumerate(copiers):
-                rows = slice(c * P // 2, (c + 1) * P // 2)
+                rows = slice(c * P // len(copiers), (c + 1) * P // len(copiers))
                 copier(dst[:, rows], src[:, rows])
             codes = held("w2_codes%d" % b, [P, PASS], U32)
             plane = held("w2_plane%d" % b, [P, PASS], U8)
@@ -122,24 +123,20 @@ def tile_list_row_servoing_kernel(
 
         v_scale_rows = held("v_scale_rows", [P, S], U8)
         nc.vector.tensor_copy(v_scale_rows[:], tab_scale_win[:].indirect(idx[:]))
-        for r in range(4):
-            nc.scalar.dma_start(
-                v_plane_moved[r:P:32, :].bitcast(I32), v_scale_rows[4 + r : P : 32, :].bitcast(I32)
-            )
-        v_plane = [v_scale_rows, v_plane_moved]
-
-        quantise_w2(1, (nc.scalar.copy, nc.vector.tensor_copy))
-
-        w3_plane = held("w3_plane", [P, N], U8, tag="tab_scale_win")
-        w3_codes = held("w3_codes", [P, h_passes, N], I32, tag="w2_raw1")
-        nc.vector.memset(w3_plane[:].bitcast(I32), 0)
-        nc.sync.dma_start(w3_codes[:], w3_words.rearrange("a p c i -> p a (c i)").bitcast(I32))
-        for q in (0, 2, 1, 3):
+        def place_v_scale_row(a, r):
             nc.sync.dma_start(
-                w3_plane[32 * q : 32 * q + 8, :].bitcast(I32),
-                w3_scales[:, 4 * q : 4 * q + 4, :].bitcast(I32),
+                v_plane[a][r:P:32, :].bitcast(I32),
+                v_scale_rows[8 * r + 4 + a : P : 32, :].bitcast(I32),
             )
 
+        v_rows = [(a, r) for a in range(k_passes) for r in range(4)]
+        for a, r in v_rows[:6]:
+            place_v_scale_row(a, r)
+        nc.sync.dma_start(tab_win[1][:], tab_words[1].rearrange("p t i -> p (t i)").bitcast(I32))
+        for a, r in v_rows[6:]:
+            place_v_scale_row(a, r)
+
+        quantise_w2(1, (nc.vector.tensor_copy,))
 
         b_sq = {}
         for b in range(h_passes):
@@ -159,21 +156,17 @@ def tile_list_row_servoing_kernel(
                     nc.scalar.activation(sq[:], bank[:], ACT.Square)
                     b_sq[(b, hf, t)] = sq
 
-        w1_err = []
-        w1_err_plane = []
-        for a in range(k_passes):
-            words = held("w1_err%d" % a, [P, H], U16)
-            nc.vector.tensor_copy(
-                words[:].rearrange("p (b t c i) -> p b c t i", b=h_passes, t=PACK, i=8),
-                w1_err_raw[:, a, :].rearrange("p (b c i t) -> p b c t i", b=h_passes, t=PACK, i=8),
-            )
-            plane = held("w1_err_plane%d" % a, [P, H], U8)
-            nc.vector.tensor_copy(
-                plane[:].rearrange("p (b t c i) -> p b c t i", b=h_passes, t=PACK, i=16),
-                w1_scale_raw[:, a, 0:H].rearrange("p (b c i t) -> p b c t i", b=h_passes, t=PACK, i=16),
-            )
-            w1_err.append(words)
-            w1_err_plane.append(plane)
+        nc.vector.tensor_copy(w1_plane[0][:, H:R].bitcast(I32), w1_scale_raw[:, H:R].bitcast(I32))
+        nc.vector.tensor_copy(
+            w1_plane[0][:, 0:H].rearrange("p (b t c i) -> p b c t i", b=h_passes, t=PACK, i=16),
+            w1_scale_raw[:, 0:H].rearrange("p (b c i t) -> p b c t i", b=h_passes, t=PACK, i=16),
+        )
+        for r in range(4):
+            nc.sync.dma_start(w1_plane[1][r:P:32, :].bitcast(I32), w1_plane[0][4 + r : P : 32, :].bitcast(I32))
+        nc.sync.dma_start(w1_err_raw[:].bitcast(I32), w1_rows[:, :, 0 : 2 * H].bitcast(I32))
+        nc.sync.dma_start(soft_sb[:], soft.rearrange("(b p t) -> p b t", p=P, t=PACK))
+        nc.sync.dma_start(w3_codes[:], w3_words.rearrange("a p c i -> p a (c i)").bitcast(I32))
+        load_two_pass_scales(w3_plane, w3_scales)
 
         v_codes = {}
         for a in range(k_passes):
@@ -184,6 +177,15 @@ def tile_list_row_servoing_kernel(
                     tab_win[a][:].bitcast(U32).indirect(idx[:, hf * list_cols : (hf + 1) * list_cols]),
                 )
                 v_codes[(a, hf)] = codes
+
+        w1_err = []
+        for a in range(k_passes):
+            words = held("w1_err%d" % a, [P, H], U16)
+            nc.vector.tensor_copy(
+                words[:].rearrange("p (b t c i) -> p b c t i", b=h_passes, t=PACK, i=8),
+                w1_err_raw[:, a, :].rearrange("p (b c i t) -> p b c t i", b=h_passes, t=PACK, i=8),
+            )
+            w1_err.append(words)
 
         def first_product(hf, codes_of, plane_of):
             bank = psum.tile([P, BANK], F32, name="bank")
@@ -204,33 +206,38 @@ def tile_list_row_servoing_kernel(
             bank = first_product(
                 hf,
                 lambda a: w1_gate[:, a, 2 * P * nt : 2 * P * (nt + 1)],
-                lambda a: w1_scale_raw[:, a, H + P * nt : H + P * (nt + 1)],
+                lambda a: w1_plane[a][:, H + P * nt : H + P * (nt + 1)],
             )
             nc.scalar.activation(gate[hf][:, nt, :], bank[:], ACT.Sigmoid)
 
         def error_bank(hf, b, t):
             cols = slice(b * PASS + t * P, b * PASS + (t + 1) * P)
-            return first_product(hf, lambda a: w1_err[a][:, cols], lambda a: w1_err_plane[a][:, cols])
+            return first_product(hf, lambda a: w1_err[a][:, cols], lambda a: w1_plane[a][:, cols])
 
         def add_terms(total, a_sq, hf, b, t):
             nc.vector.scalar_tensor_tensor(
                 total[:, t, :], a_sq, soft_sb[:, b, t : t + 1], b_sq[(b, hf, t)][:], ALU.add, ALU.add
             )
 
-        def sum_on_scalar(hf, b):
-            total = ring.tile([P, PACK, BANK], F32, name="total", bufs=3, align_bytes=64)
-            for t in range(PACK):
-                bank = error_bank(hf, b, t)
-                a_sq = ring.tile([P, BANK], F32, name="a_sq", bufs=4, align_bytes=64)
-                nc.scalar.activation(a_sq[:], bank[:], ACT.Square)
-                add_terms(total, a_sq[:], hf, b, t)
-            return total
+        def square_on_scalar(total, hf, b, t):
+            a_sq = ring.tile([P, BANK], F32, name="a_sq", bufs=4, align_bytes=64)
+            nc.scalar.activation(a_sq[:], error_bank(hf, b, t)[:], ACT.Square)
+            add_terms(total, a_sq[:], hf, b, t)
+
+        def square_on_vector(total, a_plain, hf, b):
+            count = a_plain.shape[1]
+            nc.vector.tensor_tensor(a_plain[:], a_plain[:], a_plain[:], ALU.mult)
+            for t in range(count):
+                add_terms(total, a_plain[:, t, :], hf, b, t)
+
+        def new_total():
+            return ring.tile([P, PACK, BANK], F32, name="total", bufs=4, align_bytes=64)
 
         h_codes = {}
         h_plane = {}
 
         def magnitude(hf, b, total, c0, width):
-            h_grouped = ring.tile([P, width, PACK], BF16, name="h_grouped", bufs=3, align_bytes=64)
+            h_grouped = ring.tile([P, width, PACK], BF16, name="h_grouped", bufs=4, align_bytes=64)
             nc.scalar.activation(
                 h_grouped[:].rearrange("p (c i) t -> p c t i", i=4),
                 total[:, :, c0 : c0 + width].rearrange("p t (c i) -> p c t i", i=4),
@@ -246,54 +253,67 @@ def tile_list_row_servoing_kernel(
                 h_codes[(hf, b, c)] = (codes, c - c0)
                 h_plane[(hf, b, c)] = plane
 
-        def steer(hf, c0, width):
-            per_bank = BANK // width
-            for n0 in range(0, n_tiles, per_bank):
-                bank = psum.tile([P, per_bank, width], F32, name="bank")
-                for i in range(per_bank):
-                    cols = slice((n0 + i) * P, (n0 + i + 1) * P)
-                    for b in range(h_passes):
-                        codes, at = h_codes[(hf, b, c0)]
-                        nc.tensor.matmul_mx(
-                            out=bank[:, i, :],
-                            lhsT=w3_codes[:, b, cols].bitcast(FP8X4),
-                            lhsT_scale=w3_plane[4 * b : P, cols],
-                            rhs=codes[:, at : at + width].bitcast(FP8X4),
-                            rhs_scale=h_plane[(hf, b, c0)][:, at : at + width],
-                            start=(b == 0), stop=(b == h_passes - 1),
-                        )
-                result = ring.tile([P, per_bank, width], F32, name="result", bufs=4, align_bytes=64)
-                nc.vector.tensor_tensor(
-                    result[:], bank[:], gate[hf][:, n0 : n0 + per_bank, c0 : c0 + width], ALU.mult
+        def steer_pass(b, banks, hf, c0, width):
+            per_bank = n_tiles // len(banks)
+            codes, at = h_codes[(hf, b, c0)]
+            for nt in range(n_tiles):
+                cols = slice(nt * P, (nt + 1) * P)
+                i = nt % per_bank
+                nc.tensor.matmul_mx(
+                    out=banks[nt // per_bank][:, i, :],
+                    lhsT=w3_codes[:, b, cols].bitcast(FP8X4),
+                    lhsT_scale=w3_plane[4 * b : P, cols],
+                    rhs=codes[:, at : at + width].bitcast(FP8X4),
+                    rhs_scale=h_plane[(hf, b, c0)][:, at : at + width],
+                    start=(b == 0 and i == 0), stop=(b == h_passes - 1 and i == per_bank - 1),
                 )
+
+        def open_steer(hf, c0, width, per_bank):
+            banks = [psum.tile([P, per_bank, width], F32, name="bank") for n0 in range(0, n_tiles, per_bank)]
+            steer_pass(0, banks, hf, c0, width)
+            return banks
+
+        def close_steer(banks, hf, c0, width):
+            per_bank = n_tiles // len(banks)
+            steer_pass(1, banks, hf, c0, width)
+            for k, bank in enumerate(banks):
+                n0 = k * per_bank
+                result = gate[hf][:, n0 : n0 + per_bank, c0 : c0 + width]
+                nc.vector.tensor_tensor(result, bank[:], result, ALU.mult)
                 j0 = hf * BANK + c0
                 nc.sync.dma_start(
                     out[n0 * P : (n0 + per_bank) * P, j0 : j0 + width].rearrange("(i p) j -> p i j", p=P),
-                    result[:],
+                    result,
                 )
 
-        for nt in range(n_tiles):
-            make_gate(0, nt)
-        total0 = ring.tile([P, PACK, BANK], F32, name="total", bufs=3, align_bytes=64)
-        a_plain = held("a_plain", [P, PACK, BANK], F32)
-        a_sq0 = held("a_sq0", [P, PACK, BANK], F32)
+        for hf in range(HALVES):
+            for nt in range(n_tiles):
+                make_gate(hf, nt)
+        total = {(hf, b): new_total() for hf in range(HALVES) for b in range(h_passes)}
+        a_plain = ring.tile([P, ON_VECTOR[0], BANK], F32, name="a_plain", bufs=1, align_bytes=64)
+        for t in range(ON_VECTOR[0]):
+            nc.vector.tensor_copy(a_plain[:, t, :], error_bank(0, 0, t)[:])
+        square_on_vector(total[(0, 0)], a_plain, 0, 0)
+        for t in range(ON_VECTOR[0], PACK):
+            square_on_scalar(total[(0, 0)], 0, 0, t)
         for t in range(PACK):
-            bank = error_bank(0, 0, t)
-            nc.vector.tensor_copy(a_plain[:, t, :], bank[:])
-            make_gate(1, t)
-            if t % 2 == 1:
-                pair = slice(t - 1, t + 1)
-                nc.vector.tensor_tensor(a_sq0[:, pair, :], a_plain[:, pair, :], a_plain[:, pair, :], ALU.mult)
-        for t in range(PACK):
-            add_terms(total0, a_sq0[:, t, :], 0, 0, t)
-
-        total1 = sum_on_scalar(0, 1)
-        magnitude(0, 0, total0, 0, BANK)
-        total2 = sum_on_scalar(1, 0)
-        magnitude(0, 1, total1, 0, BANK)
-        steer(0, 0, BANK)
-        total3 = sum_on_scalar(1, 1)
-        magnitude(1, 0, total2, 0, BANK)
-        for c0 in range(0, BANK, TAIL):
-            magnitude(1, 1, total3, c0, TAIL)
-            steer(1, c0, TAIL)
+            square_on_scalar(total[(0, 1)], 0, 1, t)
+        a_plain = ring.tile([P, ON_VECTOR[1], BANK], F32, name="a_plain", bufs=1, align_bytes=64)
+        for t in range(ON_VECTOR[1]):
+            nc.vector.tensor_copy(a_plain[:, t, :], error_bank(1, 0, t)[:])
+        magnitude(0, 0, total[(0, 0)], 0, BANK)
+        square_on_vector(total[(1, 0)], a_plain, 1, 0)
+        magnitude(0, 1, total[(0, 1)], 0, BANK)
+        for t in range(ON_VECTOR[1], PACK):
+            square_on_scalar(total[(1, 0)], 1, 0, t)
+        half = BANK // 2
+        for c0 in (0, half):
+            for t in range(c0 // P, c0 // P + 2):
+                square_on_scalar(total[(1, 1)], 1, 1, t)
+            magnitude(1, 0, total[(1, 0)], c0, half)
+        close_steer(open_steer(0, 0, BANK, 1), 0, 0, BANK)
+        tail = [(c0, width, open_steer(1, c0, width, per_bank)) for c0, width, per_bank in TAIL]
+        for c0, width, banks in tail:
+            magnitude(1, 1, total[(1, 1)], c0, width)
+        for c0, width, banks in tail:
+            close_steer(banks, 1, c0, width)

@@ -59,11 +59,7 @@ def tile_list_row_servoing_kernel(
         soft_sb = held("soft_sb", [P, h_passes, PACK], F32)
         v_plane = [held("v_plane%d" % a, [P, S], U8) for a in range(k_passes)]
         v2_plane = held("v2_plane", [P, S], U8)
-        warm = held("warm", [P, 1], F32)
-        warm_out = held("warm_out", [P, 1], F32)
 
-        nc.gpsimd.memset(warm[:], 0.0)
-        nc.scalar.activation(warm_out[:], warm[:], ACT.Sigmoid)
         for plane in (tab2_scale_win, tab_scale_win, w1_scale_raw, v2_plane, *v_plane, w1_plane[1], w3_plane):
             nc.vector.memset(plane[:].bitcast(I32), 0)
 

@@ -52,16 +52,20 @@ def tile_list_row_servoing_kernel(
         w2_raw = [held("w2_raw%d" % b, [P, PACK, PASS], F32) for b in range(h_passes)]
         w1_err_raw = held("w1_err_raw", [P, k_passes, H], U16)
         w1_gate = held("w1_gate", [P, k_passes, 2 * N], U8)
-        w1_scale_raw = held("w1_scale_raw", [P, R], U8)
-        w1_plane = [held("w1_plane%d" % a, [P, R], U8) for a in range(k_passes)]
+        w1_scale_raw = held("w1_scale_raw", [P, k_passes, R], U8)
+        w1_plane = [held("w1_plane%d" % a, [P, H], U8) for a in range(k_passes)]
         w3_plane = held("w3_plane", [P, N], U8)
         w3_codes = held("w3_codes", [P, h_passes, N], I32)
         soft_sb = held("soft_sb", [P, h_passes, PACK], F32)
-        v_plane = [held("v_plane%d" % a, [P, S], U8) for a in range(k_passes)]
+        v_plane = held("v_plane", [P, k_passes * S], U8)
         v2_plane = held("v2_plane", [P, S], U8)
 
-        for plane in (tab2_scale_win, tab_scale_win, w1_scale_raw, v2_plane, *v_plane, w1_plane[1], w3_plane):
-            nc.vector.memset(plane[:].bitcast(I32), 0)
+        for window in (tab2_scale_win, tab_scale_win):
+            nc.vector.memset(window[:, 0 : T // 2].bitcast(I32), 0)
+            nc.gpsimd.memset(window[:, T // 2 : T].bitcast(I32), 0)
+        nc.vector.memset(w1_scale_raw[:].bitcast(I32), 0)
+        for plane in (v2_plane, v_plane, w3_plane):
+            nc.gpsimd.memset(plane[:].bitcast(I32), 0)
 
         def load_two_pass_scales(plane, scales):
             for q in (0, 2, 1, 3):
@@ -71,24 +75,27 @@ def tile_list_row_servoing_kernel(
 
         w2_rows = w2.rearrange("(p j) r -> p j r", j=PACK)
         w1_rows = w1_words.rearrange("a p c -> p a c")
-        nc.sync.dma_start(w2_raw[0][:, :, 0 : PASS // 2], w2_rows[:, :, 0 : PASS // 2])
+        nc.sync.dma_start(w2_raw[0][:], w2_rows[:, :, 0:PASS])
         nc.sync.dma_start(idx2[:], offs2)
         nc.sync.dma_start(tab2_scale_win[4:P:8, :].bitcast(I32), tab2_scales[0].bitcast(I32))
-        nc.sync.dma_start(w2_raw[0][:, :, PASS // 2 : PASS], w2_rows[:, :, PASS // 2 : PASS])
-        nc.sync.dma_start(idx[:], offs)
-        for a in range(k_passes):
-            nc.sync.dma_start(tab_scale_win[4 + a : P : 8, :].bitcast(I32), tab_scales[a].bitcast(I32))
         nc.sync.dma_start(tab2_win[:].bitcast(I32), tab2_words[0].bitcast(I32))
-        load_two_pass_scales(w1_scale_raw, w1_scales)
+        nc.sync.dma_start(idx[:], offs)
+        nc.sync.dma_start(
+            tab_scale_win[2:P:4, :].bitcast(I32), tab_scales.rearrange("a q t -> q a t").bitcast(I32)
+        )
+        for q in (0, 2, 1, 3):
+            nc.sync.dma_start(
+                w1_scale_raw[32 * q : 32 * q + 4].bitcast(I32),
+                w1_scales[:, 4 * q : 4 * q + 4, :].rearrange("a r c -> r a c").bitcast(I32),
+            )
         nc.sync.dma_start(w2_raw[1][:], w2_rows[:, :, PASS : 2 * PASS])
 
         v2_scale_rows = held("v2_scale_rows", [P, S], U8)
         nc.vector.tensor_copy(v2_scale_rows[:], tab2_scale_win[:].indirect(idx2[:]))
         for r in range(4):
             nc.sync.dma_start(v2_plane[r:P:32, :].bitcast(I32), v2_scale_rows[8 * r + 4 : P : 32, :].bitcast(I32))
-
-        nc.sync.dma_start(w1_gate[:].bitcast(I32), w1_rows[:, :, 2 * H : 2 * R].bitcast(I32))
         nc.sync.dma_start(tab_win[0][:], tab_words[0].rearrange("p t i -> p (t i)").bitcast(I32))
+        nc.sync.dma_start(w1_gate[:].bitcast(I32), w1_rows[:, :, 2 * H : 2 * R].bitcast(I32))
 
         w2_codes = []
         w2_plane = []
@@ -109,7 +116,7 @@ def tile_list_row_servoing_kernel(
             w2_codes.append(codes)
             w2_plane.append(plane)
 
-        quantise_w2(0, (nc.scalar.copy, nc.scalar.copy))
+        quantise_w2(0, (nc.scalar.copy,))
 
         v2_codes = []
         for hf in range(HALVES):
@@ -119,18 +126,12 @@ def tile_list_row_servoing_kernel(
 
         v_scale_rows = held("v_scale_rows", [P, S], U8)
         nc.vector.tensor_copy(v_scale_rows[:], tab_scale_win[:].indirect(idx[:]))
-        def place_v_scale_row(a, r):
+        for q in (0, 2, 1, 3):
             nc.sync.dma_start(
-                v_plane[a][r:P:32, :].bitcast(I32),
-                v_scale_rows[8 * r + 4 + a : P : 32, :].bitcast(I32),
+                v_plane[32 * q : 32 * q + 4, :].bitcast(I32),
+                v_scale_rows[32 * q + 2 : 32 * q + 32 : 4, :].bitcast(I32),
             )
-
-        v_rows = [(a, r) for a in range(k_passes) for r in range(4)]
-        for a, r in v_rows[:6]:
-            place_v_scale_row(a, r)
         nc.sync.dma_start(tab_win[1][:], tab_words[1].rearrange("p t i -> p (t i)").bitcast(I32))
-        for a, r in v_rows[6:]:
-            place_v_scale_row(a, r)
 
         quantise_w2(1, (nc.vector.tensor_copy,))
 
@@ -152,13 +153,11 @@ def tile_list_row_servoing_kernel(
                     nc.scalar.activation(sq[:], bank[:], ACT.Square)
                     b_sq[(b, hf, t)] = sq
 
-        nc.vector.tensor_copy(w1_plane[0][:, H:R].bitcast(I32), w1_scale_raw[:, H:R].bitcast(I32))
-        nc.vector.tensor_copy(
-            w1_plane[0][:, 0:H].rearrange("p (b t c i) -> p b c t i", b=h_passes, t=PACK, i=16),
-            w1_scale_raw[:, 0:H].rearrange("p (b c i t) -> p b c t i", b=h_passes, t=PACK, i=16),
-        )
-        for r in range(4):
-            nc.sync.dma_start(w1_plane[1][r:P:32, :].bitcast(I32), w1_plane[0][4 + r : P : 32, :].bitcast(I32))
+        for a in range(k_passes):
+            nc.vector.tensor_copy(
+                w1_plane[a][:].rearrange("p (b t c i) -> p b c t i", b=h_passes, t=PACK, i=16),
+                w1_scale_raw[:, a, 0:H].rearrange("p (b c i t) -> p b c t i", b=h_passes, t=PACK, i=16),
+            )
         nc.sync.dma_start(w1_err_raw[:].bitcast(I32), w1_rows[:, :, 0 : 2 * H].bitcast(I32))
         nc.sync.dma_start(soft_sb[:], soft.rearrange("(b p t) -> p b t", p=P, t=PACK))
         nc.sync.dma_start(w3_codes[:], w3_words.rearrange("a p c i -> p a (c i)").bitcast(I32))
@@ -191,7 +190,7 @@ def tile_list_row_servoing_kernel(
                     lhsT=codes_of(a).bitcast(FP4X4),
                     lhsT_scale=plane_of(a),
                     rhs=v_codes[(a, hf)][:].bitcast(FP8X4),
-                    rhs_scale=v_plane[a][:, hf * BANK : (hf + 1) * BANK],
+                    rhs_scale=v_plane[:, a * S + hf * BANK : a * S + (hf + 1) * BANK],
                     start=(a == 0), stop=(a == k_passes - 1),
                 )
             return bank
@@ -202,7 +201,7 @@ def tile_list_row_servoing_kernel(
             bank = first_product(
                 hf,
                 lambda a: w1_gate[:, a, 2 * P * nt : 2 * P * (nt + 1)],
-                lambda a: w1_plane[a][:, H + P * nt : H + P * (nt + 1)],
+                lambda a: w1_scale_raw[:, a, H + P * nt : H + P * (nt + 1)],
             )
             nc.scalar.activation(gate[hf][:, nt, :], bank[:], ACT.Sigmoid)
 

@@ -50,8 +50,7 @@ def tile_list_row_servoing_kernel(
         tab_scale_win = held("tab_scale_win", [P, T], U8)
         tab2_scale_win = held("tab2_scale_win", [P, T], U8)
         w2_raw = [held("w2_raw%d" % b, [P, PACK, PASS], F32) for b in range(h_passes)]
-        w1_err_raw = held("w1_err_raw", [P, k_passes, H], U16)
-        w1_gate = held("w1_gate", [P, k_passes, 2 * N], U8)
+        w1_raw = [held("w1_raw%d" % a, [P, R], U16) for a in range(k_passes)]
         w1_scale_raw = held("w1_scale_raw", [P, k_passes, R], U8)
         w1_plane = [held("w1_plane%d" % a, [P, H], U8) for a in range(k_passes)]
         w3_plane = held("w3_plane", [P, N], U8)
@@ -59,6 +58,10 @@ def tile_list_row_servoing_kernel(
         soft_sb = held("soft_sb", [P, h_passes, PACK], F32)
         v_plane = held("v_plane", [P, k_passes * S], U8)
         v2_plane = held("v2_plane", [P, S], U8)
+
+        warm = held("warm", [P, 2], F32)
+        nc.vector.memset(warm[:, 0:1], 0.0)
+        nc.scalar.activation(warm[:, 1:2], warm[:, 0:1], ACT.Sigmoid)
 
         for window in (tab2_scale_win, tab_scale_win):
             nc.vector.memset(window[:, 0 : T // 2].bitcast(I32), 0)
@@ -74,7 +77,6 @@ def tile_list_row_servoing_kernel(
                 )
 
         w2_rows = w2.rearrange("(p j) r -> p j r", j=PACK)
-        w1_rows = w1_words.rearrange("a p c -> p a c")
         nc.sync.dma_start(w2_raw[0][:], w2_rows[:, :, 0:PASS])
         nc.sync.dma_start(idx2[:], offs2)
         nc.sync.dma_start(tab2_scale_win[4:P:8, :].bitcast(I32), tab2_scales[0].bitcast(I32))
@@ -95,7 +97,9 @@ def tile_list_row_servoing_kernel(
         for r in range(4):
             nc.sync.dma_start(v2_plane[r:P:32, :].bitcast(I32), v2_scale_rows[8 * r + 4 : P : 32, :].bitcast(I32))
         nc.sync.dma_start(tab_win[0][:], tab_words[0].rearrange("p t i -> p (t i)").bitcast(I32))
-        nc.sync.dma_start(w1_gate[:].bitcast(I32), w1_rows[:, :, 2 * H : 2 * R].bitcast(I32))
+        nc.sync.dma_start(w1_raw[0][:, H:R].bitcast(I32), w1_words[0, :, 2 * H : 2 * R].bitcast(I32))
+        last_pass = tab_words[1].rearrange("p t i -> p (t i)").bitcast(I32)
+        nc.sync.dma_start(tab_win[1][:, 0 : T // 2], last_pass[:, 0 : T // 2])
 
         w2_codes = []
         w2_plane = []
@@ -131,9 +135,9 @@ def tile_list_row_servoing_kernel(
                 v_plane[32 * q : 32 * q + 4, :].bitcast(I32),
                 v_scale_rows[32 * q + 2 : 32 * q + 32 : 4, :].bitcast(I32),
             )
-        nc.sync.dma_start(tab_win[1][:], tab_words[1].rearrange("p t i -> p (t i)").bitcast(I32))
+        nc.sync.dma_start(tab_win[1][:, T // 2 : T], last_pass[:, T // 2 : T])
 
-        quantise_w2(1, (nc.vector.tensor_copy,))
+        quantise_w2(1, (nc.scalar.copy, nc.vector.tensor_copy))
 
         b_sq = {}
         for b in range(h_passes):
@@ -158,7 +162,8 @@ def tile_list_row_servoing_kernel(
                 w1_plane[a][:].rearrange("p (b t c i) -> p b c t i", b=h_passes, t=PACK, i=16),
                 w1_scale_raw[:, a, 0:H].rearrange("p (b c i t) -> p b c t i", b=h_passes, t=PACK, i=16),
             )
-        nc.sync.dma_start(w1_err_raw[:].bitcast(I32), w1_rows[:, :, 0 : 2 * H].bitcast(I32))
+        nc.sync.dma_start(w1_raw[1][:].bitcast(I32), w1_words[1].bitcast(I32))
+        nc.sync.dma_start(w1_raw[0][:, 0:H].bitcast(I32), w1_words[0, :, 0 : 2 * H].bitcast(I32))
         nc.sync.dma_start(soft_sb[:], soft.rearrange("(b p t) -> p b t", p=P, t=PACK))
         nc.sync.dma_start(w3_codes[:], w3_words.rearrange("a p c i -> p a (c i)").bitcast(I32))
         load_two_pass_scales(w3_plane, w3_scales)
@@ -178,7 +183,7 @@ def tile_list_row_servoing_kernel(
             words = held("w1_err%d" % a, [P, H], U16)
             nc.vector.tensor_copy(
                 words[:].rearrange("p (b t c i) -> p b c t i", b=h_passes, t=PACK, i=8),
-                w1_err_raw[:, a, :].rearrange("p (b c i t) -> p b c t i", b=h_passes, t=PACK, i=8),
+                w1_raw[a][:, 0:H].rearrange("p (b c i t) -> p b c t i", b=h_passes, t=PACK, i=8),
             )
             w1_err.append(words)
 
@@ -200,7 +205,7 @@ def tile_list_row_servoing_kernel(
         def make_gate(hf, nt):
             bank = first_product(
                 hf,
-                lambda a: w1_gate[:, a, 2 * P * nt : 2 * P * (nt + 1)],
+                lambda a: w1_raw[a][:, H + P * nt : H + P * (nt + 1)],
                 lambda a: w1_scale_raw[:, a, H + P * nt : H + P * (nt + 1)],
             )
             nc.scalar.activation(gate[hf][:, nt, :], bank[:], ACT.Sigmoid)

@@ -306,14 +306,14 @@ def tile_list_row_servoing_kernel(
         magnitude(0, 1, total[(0, 1)], 0, BANK)
         for t in range(ON_VECTOR[1], PACK):
             square_on_scalar(total[(1, 0)], 1, 0, t)
-        half = BANK // 2
-        for c0 in (0, half):
-            for t in range(c0 // P, c0 // P + 2):
-                square_on_scalar(total[(1, 1)], 1, 1, t)
-            magnitude(1, 0, total[(1, 0)], c0, half)
-        close_steer(open_steer(0, 0, BANK, 1), 0, 0, BANK)
-        tail = [(c0, width, open_steer(1, c0, width, per_bank)) for c0, width, per_bank in TAIL]
-        for c0, width, banks in tail:
-            magnitude(1, 1, total[(1, 1)], c0, width)
-        for c0, width, banks in tail:
-            close_steer(banks, 1, c0, width)
+        for t in range(PACK):
+            square_on_scalar(total[(1, 1)], 1, 1, t)
+        first_half = open_steer(0, 0, BANK, 1)
+        for b in range(h_passes):
+            magnitude(1, b, total[(1, b)], *TAIL[0][:2])
+        close_steer(first_half, 0, 0, BANK)
+        for n, (c0, width, per_bank) in enumerate(TAIL):
+            if n + 1 < len(TAIL):
+                for b in range(h_passes):
+                    magnitude(1, b, total[(1, b)], *TAIL[n + 1][:2])
+            close_steer(open_steer(1, c0, width, per_bank), 1, c0, width)

@@ -59,10 +59,6 @@ def tile_list_row_servoing_kernel(
         v_plane = held("v_plane", [P, k_passes * S], U8)
         v2_plane = held("v2_plane", [P, S], U8)
 
-        warm = held("warm", [P, 2], F32)
-        nc.vector.memset(warm[:, 0:1], 0.0)
-        nc.scalar.activation(warm[:, 1:2], warm[:, 0:1], ACT.Sigmoid)
-
         for window in (tab2_scale_win, tab_scale_win):
             nc.vector.memset(window[:, 0 : T // 2].bitcast(I32), 0)
             nc.gpsimd.memset(window[:, T // 2 : T].bitcast(I32), 0)

@@ -135,6 +135,10 @@ def tile_list_row_servoing_kernel(
 
         quantise_w2(1, (nc.scalar.copy, nc.vector.tensor_copy))
 
+        def square_bank_on_vector(result, bank):
+            twice = bank[:].unsqueeze(2).to_broadcast([P, BANK, 2])
+            nc.vector.tensor_reduce(result, twice, mybir.AxisListType.X, ALU.mult)
+
         b_sq = {}
         for b in range(h_passes):
             for hf in range(HALVES):
@@ -210,21 +214,17 @@ def tile_list_row_servoing_kernel(
             cols = slice(b * PASS + t * P, b * PASS + (t + 1) * P)
             return first_product(hf, lambda a: w1_err[a][:, cols], lambda a: w1_plane[a][:, cols])
 
-        def add_terms(total, a_sq, hf, b, t):
+        def square_on_scalar(hf, b, t):
+            nc.scalar.activation(total[(hf, b)][:, t, :], error_bank(hf, b, t)[:], ACT.Square)
+
+        def square_on_vector(hf, b, t):
+            square_bank_on_vector(total[(hf, b)][:, t, :], error_bank(hf, b, t))
+
+        def add_terms(hf, b, t):
+            terms = total[(hf, b)][:, t, :]
             nc.vector.scalar_tensor_tensor(
-                total[:, t, :], a_sq, soft_sb[:, b, t : t + 1], b_sq[(b, hf, t)][:], ALU.add, ALU.add
+                terms, terms, soft_sb[:, b, t : t + 1], b_sq[(b, hf, t)][:], ALU.add, ALU.add
             )
-
-        def square_on_scalar(total, hf, b, t):
-            a_sq = ring.tile([P, BANK], F32, name="a_sq", bufs=4, align_bytes=64)
-            nc.scalar.activation(a_sq[:], error_bank(hf, b, t)[:], ACT.Square)
-            add_terms(total, a_sq[:], hf, b, t)
-
-        def square_on_vector(total, a_plain, hf, b):
-            count = a_plain.shape[1]
-            nc.vector.tensor_tensor(a_plain[:], a_plain[:], a_plain[:], ALU.mult)
-            for t in range(count):
-                add_terms(total, a_plain[:, t, :], hf, b, t)
 
         def new_total():
             return ring.tile([P, PACK, BANK], F32, name="total", bufs=4, align_bytes=64)
@@ -286,24 +286,28 @@ def tile_list_row_servoing_kernel(
             for nt in range(n_tiles):
                 make_gate(hf, nt)
         total = {(hf, b): new_total() for hf in range(HALVES) for b in range(h_passes)}
-        a_plain = ring.tile([P, ON_VECTOR[0], BANK], F32, name="a_plain", bufs=1, align_bytes=64)
         for t in range(ON_VECTOR[0]):
-            nc.vector.tensor_copy(a_plain[:, t, :], error_bank(0, 0, t)[:])
-        square_on_vector(total[(0, 0)], a_plain, 0, 0)
+            square_on_vector(0, 0, t)
+        for t in range(ON_VECTOR[0]):
+            add_terms(0, 0, t)
         for t in range(ON_VECTOR[0], PACK):
-            square_on_scalar(total[(0, 0)], 0, 0, t)
+            square_on_scalar(0, 0, t)
+            add_terms(0, 0, t)
         for t in range(PACK):
-            square_on_scalar(total[(0, 1)], 0, 1, t)
-        a_plain = ring.tile([P, ON_VECTOR[1], BANK], F32, name="a_plain", bufs=1, align_bytes=64)
+            square_on_scalar(0, 1, t)
+            add_terms(0, 1, t)
         for t in range(ON_VECTOR[1]):
-            nc.vector.tensor_copy(a_plain[:, t, :], error_bank(1, 0, t)[:])
+            square_on_vector(1, 0, t)
         magnitude(0, 0, total[(0, 0)], 0, BANK)
-        square_on_vector(total[(1, 0)], a_plain, 1, 0)
+        for t in range(ON_VECTOR[1]):
+            add_terms(1, 0, t)
         magnitude(0, 1, total[(0, 1)], 0, BANK)
         for t in range(ON_VECTOR[1], PACK):
-            square_on_scalar(total[(1, 0)], 1, 0, t)
+            square_on_scalar(1, 0, t)
+            add_terms(1, 0, t)
         for t in range(PACK):
-            square_on_scalar(total[(1, 1)], 1, 1, t)
+            square_on_scalar(1, 1, t)
+            add_terms(1, 1, t)
         first_half = open_steer(0, 0, BANK, 1)
         for b in range(h_passes):
             magnitude(1, b, total[(1, b)], *TAIL[0][:2])

@@ -21,7 +21,8 @@ PACK = 4
 PASS = P * PACK
 BANK = 512
 HALVES = S // BANK
-ON_VECTOR = (1, 3)
+ON_VECTOR = (1, 4)
+ON_GPSIMD = ((1, 0, 0), (1, 0, 1), (1, 0, 2))
 TAIL = ((0, 256, 2), (256, 128, 4), (384, 128, 2))
 
 
@@ -143,6 +144,7 @@ def tile_list_row_servoing_kernel(
         for b in range(h_passes):
             for hf in range(HALVES):
                 cols = slice(hf * BANK, (hf + 1) * BANK)
+                group = held("b_sq%d%d" % (b, hf), [P, PACK, BANK], F32)
                 for t in range(PACK):
                     bank = psum.tile([P, BANK], F32, name="bank")
                     nc.tensor.matmul_mx(
@@ -153,9 +155,8 @@ def tile_list_row_servoing_kernel(
                         rhs_scale=v2_plane[:, cols],
                         start=True, stop=True,
                     )
-                    sq = held("b_sq%d%d%d" % (b, hf, t), [P, BANK], F32)
-                    nc.scalar.activation(sq[:], bank[:], ACT.Square)
-                    b_sq[(b, hf, t)] = sq
+                    nc.scalar.activation(group[:, t, :], bank[:], ACT.Square)
+                    b_sq[(b, hf, t)] = group[:, t, :]
 
         for a in range(k_passes):
             nc.vector.tensor_copy(
@@ -186,6 +187,10 @@ def tile_list_row_servoing_kernel(
                 w1_raw[a][:, 0:H].rearrange("p (b c i t) -> p b c t i", b=h_passes, t=PACK, i=8),
             )
             w1_err.append(words)
+
+        for hf, b, t in ON_GPSIMD:
+            sq = b_sq[(b, hf, t)]
+            nc.vector.tensor_scalar_add(sq, sq, soft_sb[:, b, t : t + 1])
 
         def first_product(hf, codes_of, plane_of):
             bank = psum.tile([P, BANK], F32, name="bank")
@@ -222,9 +227,13 @@ def tile_list_row_servoing_kernel(
 
         def add_terms(hf, b, t):
             terms = total[(hf, b)][:, t, :]
-            nc.vector.scalar_tensor_tensor(
-                terms, terms, soft_sb[:, b, t : t + 1], b_sq[(b, hf, t)][:], ALU.add, ALU.add
-            )
+            result = sums[(hf, b)][:, t, :]
+            if (hf, b, t) in ON_GPSIMD:
+                nc.gpsimd.tensor_tensor(result, terms, b_sq[(b, hf, t)], ALU.add)
+            else:
+                nc.vector.scalar_tensor_tensor(
+                    result, terms, soft_sb[:, b, t : t + 1], b_sq[(b, hf, t)], ALU.add, ALU.add
+                )
 
         def new_total():
             return ring.tile([P, PACK, BANK], F32, name="total", bufs=4, align_bytes=64)
@@ -286,6 +295,7 @@ def tile_list_row_servoing_kernel(
             for nt in range(n_tiles):
                 make_gate(hf, nt)
         total = {(hf, b): new_total() for hf in range(HALVES) for b in range(h_passes)}
+        sums = dict(total)
         for t in range(ON_VECTOR[0]):
             square_on_vector(0, 0, t)
         for t in range(ON_VECTOR[0]):
@@ -299,21 +309,19 @@ def tile_list_row_servoing_kernel(
         for t in range(ON_VECTOR[1]):
             square_on_vector(1, 0, t)
         magnitude(0, 0, total[(0, 0)], 0, BANK)
-        for t in range(ON_VECTOR[1]):
-            add_terms(1, 0, t)
         magnitude(0, 1, total[(0, 1)], 0, BANK)
-        for t in range(ON_VECTOR[1], PACK):
-            square_on_scalar(1, 0, t)
+        sums[(1, 0)] = held("b_sq10", [P, PACK, BANK], F32)
+        for t in range(PACK):
             add_terms(1, 0, t)
         for t in range(PACK):
             square_on_scalar(1, 1, t)
             add_terms(1, 1, t)
         first_half = open_steer(0, 0, BANK, 1)
         for b in range(h_passes):
-            magnitude(1, b, total[(1, b)], *TAIL[0][:2])
+            magnitude(1, b, sums[(1, b)], *TAIL[0][:2])
         close_steer(first_half, 0, 0, BANK)
         for n, (c0, width, per_bank) in enumerate(TAIL):
             if n + 1 < len(TAIL):
                 for b in range(h_passes):
-                    magnitude(1, b, total[(1, b)], *TAIL[n + 1][:2])
+                    magnitude(1, b, sums[(1, b)], *TAIL[n + 1][:2])
             close_steer(open_steer(1, c0, width, per_bank), 1, c0, width)

@@ -21,8 +21,10 @@ PACK = 4
 PASS = P * PACK
 BANK = 512
 HALVES = S // BANK
-ON_VECTOR = (1, 4)
-ON_GPSIMD = ((1, 0, 0), (1, 0, 1), (1, 0, 2))
+PSUM_BANKS = 8
+QUADRANTS = (0, 2, 1, 3)
+EARLY_RUN = 2
+ON_GPSIMD = tuple((0, 0, t) for t in range(EARLY_RUN - 1)) + tuple((1, 0, t) for t in range(PACK - 1))
 TAIL = ((0, 256, 2), (256, 128, 4), (384, 128, 2))
 
 
@@ -39,7 +41,7 @@ def tile_list_row_servoing_kernel(
     with ExitStack() as ctx:
         keep = ctx.enter_context(tc.tile_pool(name="keep", bufs=1))
         ring = ctx.enter_context(tc.tile_pool(name="ring", bufs=2))
-        psum = ctx.enter_context(tc.psum_pool(name="psum", bufs=8))
+        psum = ctx.enter_context(tc.psum_pool(name="psum", bufs=PSUM_BANKS))
 
         def held(name, shape, dtype):
             return keep.tile(shape, dtype, name=name, align_bytes=64)
@@ -67,12 +69,6 @@ def tile_list_row_servoing_kernel(
         for plane in (v2_plane, v_plane, w3_plane):
             nc.gpsimd.memset(plane[:].bitcast(I32), 0)
 
-        def load_two_pass_scales(plane, scales):
-            for q in (0, 2, 1, 3):
-                nc.sync.dma_start(
-                    plane[32 * q : 32 * q + 8, :].bitcast(I32), scales[:, 4 * q : 4 * q + 4, :].bitcast(I32)
-                )
-
         w2_rows = w2.rearrange("(p j) r -> p j r", j=PACK)
         nc.sync.dma_start(w2_raw[0][:], w2_rows[:, :, 0:PASS])
         nc.sync.dma_start(idx2[:], offs2)
@@ -82,7 +78,7 @@ def tile_list_row_servoing_kernel(
         nc.sync.dma_start(
             tab_scale_win[2:P:4, :].bitcast(I32), tab_scales.rearrange("a q t -> q a t").bitcast(I32)
         )
-        for q in (0, 2, 1, 3):
+        for q in QUADRANTS:
             nc.sync.dma_start(
                 w1_scale_raw[32 * q : 32 * q + 4].bitcast(I32),
                 w1_scales[:, 4 * q : 4 * q + 4, :].rearrange("a r c -> r a c").bitcast(I32),
@@ -106,8 +102,8 @@ def tile_list_row_servoing_kernel(
             src = w2_raw[b][:].rearrange("p j (m t) -> p m j t", t=PACK)
             dst = grouped[:].rearrange("p t m j -> p m j t")
             for c, copier in enumerate(copiers):
-                rows = slice(c * P // len(copiers), (c + 1) * P // len(copiers))
-                copier(dst[:, rows], src[:, rows])
+                places = slice(c * P // len(copiers), (c + 1) * P // len(copiers))
+                copier(dst[:, places], src[:, places])
             codes = held("w2_codes%d" % b, [P, PASS], U32)
             plane = held("w2_plane%d" % b, [P, PASS], U8)
             nc.vector.quantize_mx(
@@ -127,7 +123,7 @@ def tile_list_row_servoing_kernel(
 
         v_scale_rows = held("v_scale_rows", [P, S], U8)
         nc.vector.tensor_copy(v_scale_rows[:], tab_scale_win[:].indirect(idx[:]))
-        for q in (0, 2, 1, 3):
+        for q in QUADRANTS:
             nc.sync.dma_start(
                 v_plane[32 * q : 32 * q + 4, :].bitcast(I32),
                 v_scale_rows[32 * q + 2 : 32 * q + 32 : 4, :].bitcast(I32),
@@ -136,14 +132,10 @@ def tile_list_row_servoing_kernel(
 
         quantise_w2(1, (nc.scalar.copy, nc.vector.tensor_copy))
 
-        def square_bank_on_vector(result, bank):
-            twice = bank[:].unsqueeze(2).to_broadcast([P, BANK, 2])
-            nc.vector.tensor_reduce(result, twice, mybir.AxisListType.X, ALU.mult)
-
         b_sq = {}
         for b in range(h_passes):
             for hf in range(HALVES):
-                cols = slice(hf * BANK, (hf + 1) * BANK)
+                entries = slice(hf * BANK, (hf + 1) * BANK)
                 group = held("b_sq%d%d" % (b, hf), [P, PACK, BANK], F32)
                 for t in range(PACK):
                     bank = psum.tile([P, BANK], F32, name="bank")
@@ -152,11 +144,11 @@ def tile_list_row_servoing_kernel(
                         lhsT=w2_codes[b][:, t * P : (t + 1) * P].bitcast(FP8X4),
                         lhsT_scale=w2_plane[b][:, t * P : (t + 1) * P],
                         rhs=v2_codes[hf][:].bitcast(FP4X4),
-                        rhs_scale=v2_plane[:, cols],
+                        rhs_scale=v2_plane[:, entries],
                         start=True, stop=True,
                     )
                     nc.scalar.activation(group[:, t, :], bank[:], ACT.Square)
-                    b_sq[(b, hf, t)] = group[:, t, :]
+                    b_sq[(hf, b, t)] = group[:, t, :]
 
         for a in range(k_passes):
             nc.vector.tensor_copy(
@@ -167,7 +159,10 @@ def tile_list_row_servoing_kernel(
         nc.sync.dma_start(w1_raw[0][:, 0:H].bitcast(I32), w1_words[0, :, 0 : 2 * H].bitcast(I32))
         nc.sync.dma_start(soft_sb[:], soft.rearrange("(b p t) -> p b t", p=P, t=PACK))
         nc.sync.dma_start(w3_codes[:], w3_words.rearrange("a p c i -> p a (c i)").bitcast(I32))
-        load_two_pass_scales(w3_plane, w3_scales)
+        for q in QUADRANTS:
+            nc.sync.dma_start(
+                w3_plane[32 * q : 32 * q + 8, :].bitcast(I32), w3_scales[:, 4 * q : 4 * q + 4, :].bitcast(I32)
+            )
 
         v_codes = {}
         for a in range(k_passes):
@@ -189,8 +184,7 @@ def tile_list_row_servoing_kernel(
             w1_err.append(words)
 
         for hf, b, t in ON_GPSIMD:
-            sq = b_sq[(b, hf, t)]
-            nc.vector.tensor_scalar_add(sq, sq, soft_sb[:, b, t : t + 1])
+            nc.vector.tensor_scalar_add(b_sq[(hf, b, t)], b_sq[(hf, b, t)], soft_sb[:, b, t : t + 1])
 
         def first_product(hf, codes_of, plane_of):
             bank = psum.tile([P, BANK], F32, name="bank")
@@ -216,36 +210,34 @@ def tile_list_row_servoing_kernel(
             nc.scalar.activation(gate[hf][:, nt, :], bank[:], ACT.Sigmoid)
 
         def error_bank(hf, b, t):
-            cols = slice(b * PASS + t * P, b * PASS + (t + 1) * P)
-            return first_product(hf, lambda a: w1_err[a][:, cols], lambda a: w1_plane[a][:, cols])
+            places = slice(b * PASS + t * P, b * PASS + (t + 1) * P)
+            return first_product(hf, lambda a: w1_err[a][:, places], lambda a: w1_plane[a][:, places])
 
         def square_on_scalar(hf, b, t):
-            nc.scalar.activation(total[(hf, b)][:, t, :], error_bank(hf, b, t)[:], ACT.Square)
+            nc.scalar.activation(a_sq[(hf, b)][:, t, :], error_bank(hf, b, t)[:], ACT.Square)
 
         def square_on_vector(hf, b, t):
-            square_bank_on_vector(total[(hf, b)][:, t, :], error_bank(hf, b, t))
+            twice = error_bank(hf, b, t)[:].unsqueeze(2).to_broadcast([P, BANK, 2])
+            nc.vector.tensor_reduce(a_sq[(hf, b)][:, t, :], twice, mybir.AxisListType.X, ALU.mult)
 
         def add_terms(hf, b, t):
-            terms = total[(hf, b)][:, t, :]
-            result = sums[(hf, b)][:, t, :]
+            squares = a_sq[(hf, b)][:, t, :]
+            total = sums[(hf, b)][:, t, :]
             if (hf, b, t) in ON_GPSIMD:
-                nc.gpsimd.tensor_tensor(result, terms, b_sq[(b, hf, t)], ALU.add)
+                nc.gpsimd.tensor_tensor(total, squares, b_sq[(hf, b, t)], ALU.add)
             else:
                 nc.vector.scalar_tensor_tensor(
-                    result, terms, soft_sb[:, b, t : t + 1], b_sq[(b, hf, t)], ALU.add, ALU.add
+                    total, squares, soft_sb[:, b, t : t + 1], b_sq[(hf, b, t)], ALU.add, ALU.add
                 )
-
-        def new_total():
-            return ring.tile([P, PACK, BANK], F32, name="total", bufs=4, align_bytes=64)
 
         h_codes = {}
         h_plane = {}
 
-        def magnitude(hf, b, total, c0, width):
+        def magnitude(hf, b, c0, width):
             h_grouped = ring.tile([P, width, PACK], BF16, name="h_grouped", bufs=4, align_bytes=64)
             nc.scalar.activation(
                 h_grouped[:].rearrange("p (c i) t -> p c t i", i=4),
-                total[:, :, c0 : c0 + width].rearrange("p t (c i) -> p c t i", i=4),
+                sums[(hf, b)][:, :, c0 : c0 + width].rearrange("p t (c i) -> p c t i", i=4),
                 ACT.Sqrt,
             )
             codes = held("h_codes%d%d_%d" % (hf, b, c0), [P, width], U32)
@@ -254,33 +246,31 @@ def tile_list_row_servoing_kernel(
                 out=codes[:].bitcast(FP8X4), scales=plane[:],
                 in_=h_grouped[:].rearrange("p j t -> p (j t)"),
             )
-            for c in range(c0, c0 + width, P):
-                h_codes[(hf, b, c)] = (codes, c - c0)
-                h_plane[(hf, b, c)] = plane
+            h_codes[(hf, b, c0)] = codes
+            h_plane[(hf, b, c0)] = plane
 
-        def steer_pass(b, banks, hf, c0, width):
+        def steer_pass(b, banks, hf, c0):
             per_bank = n_tiles // len(banks)
-            codes, at = h_codes[(hf, b, c0)]
             for nt in range(n_tiles):
-                cols = slice(nt * P, (nt + 1) * P)
+                rows = slice(nt * P, (nt + 1) * P)
                 i = nt % per_bank
                 nc.tensor.matmul_mx(
                     out=banks[nt // per_bank][:, i, :],
-                    lhsT=w3_codes[:, b, cols].bitcast(FP8X4),
-                    lhsT_scale=w3_plane[4 * b : P, cols],
-                    rhs=codes[:, at : at + width].bitcast(FP8X4),
-                    rhs_scale=h_plane[(hf, b, c0)][:, at : at + width],
+                    lhsT=w3_codes[:, b, rows].bitcast(FP8X4),
+                    lhsT_scale=w3_plane[4 * b : P, rows],
+                    rhs=h_codes[(hf, b, c0)][:].bitcast(FP8X4),
+                    rhs_scale=h_plane[(hf, b, c0)][:],
                     start=(b == 0 and i == 0), stop=(b == h_passes - 1 and i == per_bank - 1),
                 )
 
         def open_steer(hf, c0, width, per_bank):
             banks = [psum.tile([P, per_bank, width], F32, name="bank") for n0 in range(0, n_tiles, per_bank)]
-            steer_pass(0, banks, hf, c0, width)
+            steer_pass(0, banks, hf, c0)
             return banks
 
         def close_steer(banks, hf, c0, width):
             per_bank = n_tiles // len(banks)
-            steer_pass(1, banks, hf, c0, width)
+            steer_pass(1, banks, hf, c0)
             for k, bank in enumerate(banks):
                 n0 = k * per_bank
                 result = gate[hf][:, n0 : n0 + per_bank, c0 : c0 + width]
@@ -294,23 +284,26 @@ def tile_list_row_servoing_kernel(
         for hf in range(HALVES):
             for nt in range(n_tiles):
                 make_gate(hf, nt)
-        total = {(hf, b): new_total() for hf in range(HALVES) for b in range(h_passes)}
-        sums = dict(total)
-        for t in range(ON_VECTOR[0]):
+        groups = [(hf, b) for hf in range(HALVES) for b in range(h_passes)]
+        a_sq = {
+            g: ring.tile([P, PACK, BANK], F32, name="total", bufs=len(groups), align_bytes=64) for g in groups
+        }
+        sums = dict(a_sq)
+        for t in range(EARLY_RUN):
             square_on_vector(0, 0, t)
-        for t in range(ON_VECTOR[0]):
+        for t in range(EARLY_RUN):
             add_terms(0, 0, t)
-        for t in range(ON_VECTOR[0], PACK):
+        for t in range(EARLY_RUN, PACK):
             square_on_scalar(0, 0, t)
             add_terms(0, 0, t)
         for t in range(PACK):
             square_on_scalar(0, 1, t)
             add_terms(0, 1, t)
-        for t in range(ON_VECTOR[1]):
+        for t in range(PACK):
             square_on_vector(1, 0, t)
-        magnitude(0, 0, total[(0, 0)], 0, BANK)
-        magnitude(0, 1, total[(0, 1)], 0, BANK)
+        magnitude(0, 0, 0, BANK)
         sums[(1, 0)] = held("b_sq10", [P, PACK, BANK], F32)
+        magnitude(0, 1, 0, BANK)
         for t in range(PACK):
             add_terms(1, 0, t)
         for t in range(PACK):
@@ -318,10 +311,10 @@ def tile_list_row_servoing_kernel(
             add_terms(1, 1, t)
         first_half = open_steer(0, 0, BANK, 1)
         for b in range(h_passes):
-            magnitude(1, b, sums[(1, b)], *TAIL[0][:2])
+            magnitude(1, b, *TAIL[0][:2])
         close_steer(first_half, 0, 0, BANK)
         for n, (c0, width, per_bank) in enumerate(TAIL):
             if n + 1 < len(TAIL):
                 for b in range(h_passes):
-                    magnitude(1, b, sums[(1, b)], *TAIL[n + 1][:2])
+                    magnitude(1, b, *TAIL[n + 1][:2])
             close_steer(open_steer(1, c0, width, per_bank), 1, c0, width)

@@ -24,7 +24,7 @@ HALVES = S // BANK
 PSUM_BANKS = 8
 QUADRANTS = (0, 2, 1, 3)
 EARLY_RUN = 2
-ON_GPSIMD = tuple((0, 0, t) for t in range(EARLY_RUN - 1)) + tuple((1, 0, t) for t in range(PACK - 1))
+ON_GPSIMD = tuple((0, 0, t) for t in range(EARLY_RUN - 1)) + tuple((1, 0, t) for t in range(PACK - 2))
 TAIL = ((0, 256, 2), (256, 128, 4), (384, 128, 2))
 
 

@@ -23,9 +23,10 @@ BANK = 512
 HALVES = S // BANK
 PSUM_BANKS = 8
 QUADRANTS = (0, 2, 1, 3)
-EARLY_RUN = 2
-ON_GPSIMD = tuple((0, 0, t) for t in range(EARLY_RUN - 1)) + tuple((1, 0, t) for t in range(PACK - 2))
-TAIL = ((0, 256, 2), (256, 128, 4), (384, 128, 2))
+EARLY_RUN = 3
+LATE_RUN = 3
+ON_GPSIMD = {(0, 0, 0): BANK, (0, 0, 1): BANK // 2, (1, 0, 0): BANK, (1, 0, 1): BANK // 2}
+TAIL = ((0, 256, (4, 5)), (256, 128, (6,)), (384, 128, (0, 7)))
 
 
 def tile_list_row_servoing_kernel(
@@ -41,10 +42,13 @@ def tile_list_row_servoing_kernel(
     with ExitStack() as ctx:
         keep = ctx.enter_context(tc.tile_pool(name="keep", bufs=1))
         ring = ctx.enter_context(tc.tile_pool(name="ring", bufs=2))
-        psum = ctx.enter_context(tc.psum_pool(name="psum", bufs=PSUM_BANKS))
+        psum = ctx.enter_context(tc.psum_pool(name="psum", bufs=1))
 
         def held(name, shape, dtype):
             return keep.tile(shape, dtype, name=name, align_bytes=64)
+
+        def bank_tile(n, shape):
+            return psum.tile(shape, F32, name="bank%d" % n)
 
         idx = held("idx", [P, S // 16], U16)
         idx2 = held("idx2", [P, S // 16], U16)
@@ -91,6 +95,7 @@ def tile_list_row_servoing_kernel(
             nc.sync.dma_start(v2_plane[r:P:32, :].bitcast(I32), v2_scale_rows[8 * r + 4 : P : 32, :].bitcast(I32))
         nc.sync.dma_start(tab_win[0][:], tab_words[0].rearrange("p t i -> p (t i)").bitcast(I32))
         nc.sync.dma_start(w1_raw[0][:, H:R].bitcast(I32), w1_words[0, :, 2 * H : 2 * R].bitcast(I32))
+        nc.sync.dma_start(soft_sb[:], soft.rearrange("(b p t) -> p b t", p=P, t=PACK))
         last_pass = tab_words[1].rearrange("p t i -> p (t i)").bitcast(I32)
         nc.sync.dma_start(tab_win[1][:, 0 : T // 2], last_pass[:, 0 : T // 2])
 
@@ -138,7 +143,7 @@ def tile_list_row_servoing_kernel(
                 entries = slice(hf * BANK, (hf + 1) * BANK)
                 group = held("b_sq%d%d" % (b, hf), [P, PACK, BANK], F32)
                 for t in range(PACK):
-                    bank = psum.tile([P, BANK], F32, name="bank")
+                    bank = bank_tile(PACK * hf + t, [P, BANK])
                     nc.tensor.matmul_mx(
                         out=bank[:],
                         lhsT=w2_codes[b][:, t * P : (t + 1) * P].bitcast(FP8X4),
@@ -157,7 +162,6 @@ def tile_list_row_servoing_kernel(
             )
         nc.sync.dma_start(w1_raw[1][:].bitcast(I32), w1_words[1].bitcast(I32))
         nc.sync.dma_start(w1_raw[0][:, 0:H].bitcast(I32), w1_words[0, :, 0 : 2 * H].bitcast(I32))
-        nc.sync.dma_start(soft_sb[:], soft.rearrange("(b p t) -> p b t", p=P, t=PACK))
         nc.sync.dma_start(w3_codes[:], w3_words.rearrange("a p c i -> p a (c i)").bitcast(I32))
         for q in QUADRANTS:
             nc.sync.dma_start(
@@ -165,29 +169,38 @@ def tile_list_row_servoing_kernel(
             )
 
         v_codes = {}
-        for a in range(k_passes):
-            for hf in range(HALVES):
-                codes = held("v_codes%d%d" % (a, hf), [P, BANK], U32)
-                nc.vector.tensor_copy(
-                    codes[:],
-                    tab_win[a][:].bitcast(U32).indirect(idx[:, hf * list_cols : (hf + 1) * list_cols]),
-                )
-                v_codes[(a, hf)] = codes
 
-        w1_err = []
-        for a in range(k_passes):
-            words = held("w1_err%d" % a, [P, H], U16)
+        def gather_words(a, hf, codes):
             nc.vector.tensor_copy(
-                words[:].rearrange("p (b t c i) -> p b c t i", b=h_passes, t=PACK, i=8),
-                w1_raw[a][:, 0:H].rearrange("p (b c i t) -> p b c t i", b=h_passes, t=PACK, i=8),
+                codes[:], tab_win[a][:].bitcast(U32).indirect(idx[:, hf * list_cols : (hf + 1) * list_cols])
             )
-            w1_err.append(words)
+            v_codes[(a, hf)] = codes
 
-        for hf, b, t in ON_GPSIMD:
-            nc.vector.tensor_scalar_add(b_sq[(hf, b, t)], b_sq[(hf, b, t)], soft_sb[:, b, t : t + 1])
+        for hf in range(HALVES):
+            gather_words(0, hf, held("v_first%d" % hf, [P, BANK], U32))
 
-        def first_product(hf, codes_of, plane_of):
-            bank = psum.tile([P, BANK], F32, name="bank")
+        for (hf, b, t), width in ON_GPSIMD.items():
+            terms = b_sq[(hf, b, t)][:, 0:width]
+            nc.vector.tensor_scalar_add(terms, terms, soft_sb[:, b, t : t + 1])
+
+        err_words = []
+
+        def deal_words(b):
+            words = held("err_words%d" % b, [P, k_passes, PASS], U16)
+            for a in range(k_passes):
+                nc.vector.tensor_copy(
+                    words[:, a, :].rearrange("p (t c i) -> p c t i", t=PACK, i=8),
+                    w1_raw[a][:, b * PASS : (b + 1) * PASS].rearrange("p (c i t) -> p c t i", t=PACK, i=8),
+                )
+            err_words.append(words)
+
+        gather_words(1, 0, held("v_last0", [P, BANK], U32))
+        gather_words(1, 1, held("v_last1", [P, BANK], U32))
+        deal_words(0)
+        deal_words(1)
+
+        def first_product(number, hf, codes_of, plane_of):
+            bank = bank_tile(number, [P, BANK])
             for a in range(k_passes):
                 nc.tensor.matmul_mx(
                     out=bank[:],
@@ -203,7 +216,7 @@ def tile_list_row_servoing_kernel(
 
         def make_gate(hf, nt):
             bank = first_product(
-                hf,
+                (n_tiles * hf + nt) % 7, hf,
                 lambda a: w1_raw[a][:, H + P * nt : H + P * (nt + 1)],
                 lambda a: w1_scale_raw[:, a, H + P * nt : H + P * (nt + 1)],
             )
@@ -211,7 +224,10 @@ def tile_list_row_servoing_kernel(
 
         def error_bank(hf, b, t):
             places = slice(b * PASS + t * P, b * PASS + (t + 1) * P)
-            return first_product(hf, lambda a: w1_err[a][:, places], lambda a: w1_plane[a][:, places])
+            number = (7, 1, 2, 3, 4, 5, 6, 0)[4 * b + t]
+            return first_product(
+                number, hf, lambda a: err_words[b][:, a, t * P : (t + 1) * P], lambda a: w1_plane[a][:, places]
+            )
 
         def square_on_scalar(hf, b, t):
             nc.scalar.activation(a_sq[(hf, b)][:, t, :], error_bank(hf, b, t)[:], ACT.Square)
@@ -223,11 +239,14 @@ def tile_list_row_servoing_kernel(
         def add_terms(hf, b, t):
             squares = a_sq[(hf, b)][:, t, :]
             total = sums[(hf, b)][:, t, :]
-            if (hf, b, t) in ON_GPSIMD:
-                nc.gpsimd.tensor_tensor(total, squares, b_sq[(hf, b, t)], ALU.add)
-            else:
+            terms = b_sq[(hf, b, t)]
+            split = ON_GPSIMD.get((hf, b, t), 0)
+            if split > 0:
+                nc.gpsimd.tensor_tensor(total[:, 0:split], squares[:, 0:split], terms[:, 0:split], ALU.add)
+            if split < BANK:
                 nc.vector.scalar_tensor_tensor(
-                    total, squares, soft_sb[:, b, t : t + 1], b_sq[(hf, b, t)], ALU.add, ALU.add
+                    total[:, split:BANK], squares[:, split:BANK], soft_sb[:, b, t : t + 1],
+                    terms[:, split:BANK], ALU.add, ALU.add,
                 )
 
         h_codes = {}
@@ -263,8 +282,8 @@ def tile_list_row_servoing_kernel(
                     start=(b == 0 and i == 0), stop=(b == h_passes - 1 and i == per_bank - 1),
                 )
 
-        def open_steer(hf, c0, width, per_bank):
-            banks = [psum.tile([P, per_bank, width], F32, name="bank") for n0 in range(0, n_tiles, per_bank)]
+        def open_steer(hf, c0, width, numbers):
+            banks = [bank_tile(n, [P, n_tiles // len(numbers), width]) for n in numbers]
             steer_pass(0, banks, hf, c0)
             return banks
 
@@ -281,15 +300,19 @@ def tile_list_row_servoing_kernel(
                     result,
                 )
 
-        for hf in range(HALVES):
-            for nt in range(n_tiles):
-                make_gate(hf, nt)
+        for nt in range(n_tiles):
+            make_gate(0, nt)
+        make_gate(1, 0)
+        make_gate(1, 1)
+        make_gate(1, 2)
         groups = [(hf, b) for hf in range(HALVES) for b in range(h_passes)]
         a_sq = {
             g: ring.tile([P, PACK, BANK], F32, name="total", bufs=len(groups), align_bytes=64) for g in groups
         }
         sums = dict(a_sq)
-        for t in range(EARLY_RUN):
+        square_on_vector(0, 0, 0)
+        make_gate(1, 3)
+        for t in range(1, EARLY_RUN):
             square_on_vector(0, 0, t)
         for t in range(EARLY_RUN):
             add_terms(0, 0, t)
@@ -299,22 +322,24 @@ def tile_list_row_servoing_kernel(
         for t in range(PACK):
             square_on_scalar(0, 1, t)
             add_terms(0, 1, t)
-        for t in range(PACK):
+        for t in range(LATE_RUN):
             square_on_vector(1, 0, t)
         magnitude(0, 0, 0, BANK)
         sums[(1, 0)] = held("b_sq10", [P, PACK, BANK], F32)
         magnitude(0, 1, 0, BANK)
+        for t in range(LATE_RUN, PACK):
+            square_on_scalar(1, 0, t)
         for t in range(PACK):
             add_terms(1, 0, t)
         for t in range(PACK):
             square_on_scalar(1, 1, t)
             add_terms(1, 1, t)
-        first_half = open_steer(0, 0, BANK, 1)
+        first_half = open_steer(0, 0, BANK, (7, 1, 2, 3))
         for b in range(h_passes):
             magnitude(1, b, *TAIL[0][:2])
         close_steer(first_half, 0, 0, BANK)
-        for n, (c0, width, per_bank) in enumerate(TAIL):
+        for n, (c0, width, numbers) in enumerate(TAIL):
             if n + 1 < len(TAIL):
                 for b in range(h_passes):
                     magnitude(1, b, *TAIL[n + 1][:2])
-            close_steer(open_steer(1, c0, width, per_bank), 1, c0, width)
+            close_steer(open_steer(1, c0, width, numbers), 1, c0, width)

@@ -22,6 +22,7 @@ PASS = P * PACK
 BANK = 512
 HALVES = S // BANK
 PSUM_BANKS = 8
+SPLIT = 3 * T // 8
 QUADRANTS = (0, 2, 1, 3)
 EARLY_RUN = 3
 LATE_RUN = 3
@@ -94,10 +95,9 @@ def tile_list_row_servoing_kernel(
         for r in range(4):
             nc.sync.dma_start(v2_plane[r:P:32, :].bitcast(I32), v2_scale_rows[8 * r + 4 : P : 32, :].bitcast(I32))
         nc.sync.dma_start(tab_win[0][:], tab_words[0].rearrange("p t i -> p (t i)").bitcast(I32))
-        nc.sync.dma_start(w1_raw[0][:, H:R].bitcast(I32), w1_words[0, :, 2 * H : 2 * R].bitcast(I32))
         nc.sync.dma_start(soft_sb[:], soft.rearrange("(b p t) -> p b t", p=P, t=PACK))
         last_pass = tab_words[1].rearrange("p t i -> p (t i)").bitcast(I32)
-        nc.sync.dma_start(tab_win[1][:, 0 : T // 2], last_pass[:, 0 : T // 2])
+        nc.sync.dma_start(tab_win[1][:, 0:SPLIT], last_pass[:, 0:SPLIT])
 
         w2_codes = []
         w2_plane = []
@@ -133,7 +133,8 @@ def tile_list_row_servoing_kernel(
                 v_plane[32 * q : 32 * q + 4, :].bitcast(I32),
                 v_scale_rows[32 * q + 2 : 32 * q + 32 : 4, :].bitcast(I32),
             )
-        nc.sync.dma_start(tab_win[1][:, T // 2 : T], last_pass[:, T // 2 : T])
+        nc.sync.dma_start(w1_raw[0][:, H:R].bitcast(I32), w1_words[0, :, 2 * H : 2 * R].bitcast(I32))
+        nc.sync.dma_start(tab_win[1][:, SPLIT:T], last_pass[:, SPLIT:T])
 
         quantise_w2(1, (nc.scalar.copy, nc.vector.tensor_copy))
 

@@ -22,11 +22,12 @@ PASS = P * PACK
 BANK = 512
 HALVES = S // BANK
 PSUM_BANKS = 8
+PIECE = BANK // 2
 SPLIT = 3 * T // 8
 QUADRANTS = (0, 2, 1, 3)
 EARLY_RUN = 3
-LATE_RUN = 3
-ON_GPSIMD = {(0, 0, 0): BANK, (0, 0, 1): BANK // 2, (1, 0, 0): BANK, (1, 0, 1): BANK // 2}
+LATE_RUN = 2
+ON_GPSIMD = {(0, 0, 0): BANK, (0, 0, 1): BANK // 2, (1, 0, 0): BANK // 2}
 TAIL = ((0, 256, (4, 5)), (256, 128, (6,)), (384, 128, (0, 7)))
 
 
@@ -73,6 +74,10 @@ def tile_list_row_servoing_kernel(
         nc.vector.memset(w1_scale_raw[:].bitcast(I32), 0)
         for plane in (v2_plane, v_plane, w3_plane):
             nc.gpsimd.memset(plane[:].bitcast(I32), 0)
+
+        warm = held("warm", [P, 2], F32)
+        nc.gpsimd.memset(warm[:, 0:1], 0.0)
+        nc.scalar.activation(warm[:, 1:2], warm[:, 0:1], ACT.Sigmoid)
 
         w2_rows = w2.rearrange("(p j) r -> p j r", j=PACK)
         nc.sync.dma_start(w2_raw[0][:], w2_rows[:, :, 0:PASS])
@@ -195,7 +200,12 @@ def tile_list_row_servoing_kernel(
                 )
             err_words.append(words)
 
-        gather_words(1, 0, held("v_last0", [P, BANK], U32))
+        v_codes[(1, 0)] = held("v_last0", [P, BANK], U32)
+        for c0 in range(0, BANK, PIECE):
+            nc.vector.tensor_copy(
+                v_codes[(1, 0)][:, c0 : c0 + PIECE],
+                tab_win[1][:].bitcast(U32).indirect(idx[:, c0 // 16 : (c0 + PIECE) // 16]),
+            )
         gather_words(1, 1, held("v_last1", [P, BANK], U32))
         deal_words(0)
         deal_words(1)
@@ -222,6 +232,21 @@ def tile_list_row_servoing_kernel(
                 lambda a: w1_scale_raw[:, a, H + P * nt : H + P * (nt + 1)],
             )
             nc.scalar.activation(gate[hf][:, nt, :], bank[:], ACT.Sigmoid)
+
+        def make_first_gate(c0, n0):
+            bank = bank_tile(2 * (c0 // PIECE) + n0 // 2, [P, 2, PIECE])
+            for a in range(k_passes):
+                for i in range(2):
+                    cols = slice(H + P * (n0 + i), H + P * (n0 + i + 1))
+                    nc.tensor.matmul_mx(
+                        out=bank[:, i, :],
+                        lhsT=w1_raw[a][:, cols].bitcast(FP4X4),
+                        lhsT_scale=w1_scale_raw[:, a, cols],
+                        rhs=v_codes[(a, 0)][:, c0 : c0 + PIECE].bitcast(FP8X4),
+                        rhs_scale=v_plane[:, a * S + c0 : a * S + c0 + PIECE],
+                        start=(a == 0 and i == 0), stop=(a == k_passes - 1 and i == 1),
+                    )
+            nc.scalar.activation(gate[0][:, n0 : n0 + 2, c0 : c0 + PIECE], bank[:], ACT.Sigmoid)
 
         def error_bank(hf, b, t):
             places = slice(b * PASS + t * P, b * PASS + (t + 1) * P)
@@ -301,8 +326,9 @@ def tile_list_row_servoing_kernel(
                     result,
                 )
 
-        for nt in range(n_tiles):
-            make_gate(0, nt)
+        for c0 in range(0, BANK, PIECE):
+            for n0 in range(0, n_tiles, 2):
+                make_first_gate(c0, n0)
         make_gate(1, 0)
         make_gate(1, 1)
         make_gate(1, 2)
@@ -313,6 +339,7 @@ def tile_list_row_servoing_kernel(
         sums = dict(a_sq)
         square_on_vector(0, 0, 0)
         make_gate(1, 3)
+        nc.scalar.activation(warm[:, 1:2], gate[1][:, 3, 0:1], ACT.Sqrt)
         for t in range(1, EARLY_RUN):
             square_on_vector(0, 0, t)
         for t in range(EARLY_RUN):

@@ -25,10 +25,12 @@ PSUM_BANKS = 8
 PIECE = BANK // 2
 SPLIT = 3 * T // 8
 QUADRANTS = (0, 2, 1, 3)
+GATES_AHEAD = PSUM_BANKS - 1
+ERROR_BANKS = (GATES_AHEAD,) + tuple(range(1, GATES_AHEAD)) + (0,)
 EARLY_RUN = 3
 LATE_RUN = 2
 ON_GPSIMD = {(0, 0, 0): BANK, (0, 0, 1): BANK // 2, (1, 0, 0): BANK // 2}
-TAIL = ((0, 256, (4, 5)), (256, 128, (6,)), (384, 128, (0, 7)))
+TAIL = ((0, 256, ERROR_BANKS[4:6]), (256, 128, ERROR_BANKS[6:7]), (384, 128, (ERROR_BANKS[7], ERROR_BANKS[0])))
 
 
 def tile_list_row_servoing_kernel(
@@ -43,14 +45,14 @@ def tile_list_row_servoing_kernel(
 
     with ExitStack() as ctx:
         keep = ctx.enter_context(tc.tile_pool(name="keep", bufs=1))
-        ring = ctx.enter_context(tc.tile_pool(name="ring", bufs=2))
+        ring = ctx.enter_context(tc.tile_pool(name="ring", bufs=4))
         psum = ctx.enter_context(tc.psum_pool(name="psum", bufs=1))
 
         def held(name, shape, dtype):
-            return keep.tile(shape, dtype, name=name, align_bytes=64)
+            return keep.tile(shape, dtype, name=name, align_bytes=256)
 
-        def bank_tile(n, shape):
-            return psum.tile(shape, F32, name="bank%d" % n)
+        def bank_tile(number, shape):
+            return psum.tile(shape, F32, name="bank%d" % number)
 
         idx = held("idx", [P, S // 16], U16)
         idx2 = held("idx2", [P, S // 16], U16)
@@ -176,22 +178,28 @@ def tile_list_row_servoing_kernel(
 
         v_codes = {}
 
-        def gather_words(a, hf, codes):
-            nc.vector.tensor_copy(
-                codes[:], tab_win[a][:].bitcast(U32).indirect(idx[:, hf * list_cols : (hf + 1) * list_cols])
-            )
+        def gather_words(a, hf, width):
+            codes = held("v_codes%d%d" % (a, hf), [P, BANK], U32)
+            for c0 in range(0, BANK, width):
+                j0 = hf * BANK + c0
+                nc.vector.tensor_copy(
+                    codes[:, c0 : c0 + width],
+                    tab_win[a][:].bitcast(U32).indirect(idx[:, j0 // 16 : (j0 + width) // 16]),
+                )
             v_codes[(a, hf)] = codes
 
         for hf in range(HALVES):
-            gather_words(0, hf, held("v_first%d" % hf, [P, BANK], U32))
+            gather_words(0, hf, BANK)
 
         for (hf, b, t), width in ON_GPSIMD.items():
             terms = b_sq[(hf, b, t)][:, 0:width]
             nc.vector.tensor_scalar_add(terms, terms, soft_sb[:, b, t : t + 1])
 
-        err_words = []
+        gather_words(1, 0, PIECE)
+        gather_words(1, 1, BANK)
 
-        def deal_words(b):
+        err_words = []
+        for b in range(h_passes):
             words = held("err_words%d" % b, [P, k_passes, PASS], U16)
             for a in range(k_passes):
                 nc.vector.tensor_copy(
@@ -200,60 +208,40 @@ def tile_list_row_servoing_kernel(
                 )
             err_words.append(words)
 
-        v_codes[(1, 0)] = held("v_last0", [P, BANK], U32)
-        for c0 in range(0, BANK, PIECE):
-            nc.vector.tensor_copy(
-                v_codes[(1, 0)][:, c0 : c0 + PIECE],
-                tab_win[1][:].bitcast(U32).indirect(idx[:, c0 // 16 : (c0 + PIECE) // 16]),
+        def first_pass(sums_out, a, hf, c0, width, codes, plane, start, stop):
+            j0 = a * S + hf * BANK + c0
+            nc.tensor.matmul_mx(
+                out=sums_out,
+                lhsT=codes.bitcast(FP4X4),
+                lhsT_scale=plane,
+                rhs=v_codes[(a, hf)][:, c0 : c0 + width].bitcast(FP8X4),
+                rhs_scale=v_plane[:, j0 : j0 + width],
+                start=start, stop=stop,
             )
-        gather_words(1, 1, held("v_last1", [P, BANK], U32))
-        deal_words(0)
-        deal_words(1)
-
-        def first_product(number, hf, codes_of, plane_of):
-            bank = bank_tile(number, [P, BANK])
-            for a in range(k_passes):
-                nc.tensor.matmul_mx(
-                    out=bank[:],
-                    lhsT=codes_of(a).bitcast(FP4X4),
-                    lhsT_scale=plane_of(a),
-                    rhs=v_codes[(a, hf)][:].bitcast(FP8X4),
-                    rhs_scale=v_plane[:, a * S + hf * BANK : a * S + (hf + 1) * BANK],
-                    start=(a == 0), stop=(a == k_passes - 1),
-                )
-            return bank
 
         gate = [held("gate%d" % hf, [P, n_tiles, BANK], F32) for hf in range(HALVES)]
 
-        def make_gate(hf, nt):
-            bank = first_product(
-                (n_tiles * hf + nt) % 7, hf,
-                lambda a: w1_raw[a][:, H + P * nt : H + P * (nt + 1)],
-                lambda a: w1_scale_raw[:, a, H + P * nt : H + P * (nt + 1)],
-            )
-            nc.scalar.activation(gate[hf][:, nt, :], bank[:], ACT.Sigmoid)
-
-        def make_first_gate(c0, n0):
-            bank = bank_tile(2 * (c0 // PIECE) + n0 // 2, [P, 2, PIECE])
+        def make_gate(number, hf, c0, width, n0):
+            per_bank = BANK // width
+            bank = bank_tile(number, [P, per_bank, width])
             for a in range(k_passes):
-                for i in range(2):
+                for i in range(per_bank):
                     cols = slice(H + P * (n0 + i), H + P * (n0 + i + 1))
-                    nc.tensor.matmul_mx(
-                        out=bank[:, i, :],
-                        lhsT=w1_raw[a][:, cols].bitcast(FP4X4),
-                        lhsT_scale=w1_scale_raw[:, a, cols],
-                        rhs=v_codes[(a, 0)][:, c0 : c0 + PIECE].bitcast(FP8X4),
-                        rhs_scale=v_plane[:, a * S + c0 : a * S + c0 + PIECE],
-                        start=(a == 0 and i == 0), stop=(a == k_passes - 1 and i == 1),
+                    first_pass(
+                        bank[:, i, :], a, hf, c0, width, w1_raw[a][:, cols], w1_scale_raw[:, a, cols],
+                        a == 0 and i == 0, a == k_passes - 1 and i == per_bank - 1,
                     )
-            nc.scalar.activation(gate[0][:, n0 : n0 + 2, c0 : c0 + PIECE], bank[:], ACT.Sigmoid)
+            nc.scalar.activation(gate[hf][:, n0 : n0 + per_bank, c0 : c0 + width], bank[:], ACT.Sigmoid)
 
         def error_bank(hf, b, t):
-            places = slice(b * PASS + t * P, b * PASS + (t + 1) * P)
-            number = (7, 1, 2, 3, 4, 5, 6, 0)[4 * b + t]
-            return first_product(
-                number, hf, lambda a: err_words[b][:, a, t * P : (t + 1) * P], lambda a: w1_plane[a][:, places]
-            )
+            bank = bank_tile(ERROR_BANKS[PACK * b + t], [P, BANK])
+            for a in range(k_passes):
+                first_pass(
+                    bank[:], a, hf, 0, BANK, err_words[b][:, a, t * P : (t + 1) * P],
+                    w1_plane[a][:, b * PASS + t * P : b * PASS + (t + 1) * P],
+                    a == 0, a == k_passes - 1,
+                )
+            return bank
 
         def square_on_scalar(hf, b, t):
             nc.scalar.activation(a_sq[(hf, b)][:, t, :], error_bank(hf, b, t)[:], ACT.Square)
@@ -309,7 +297,7 @@ def tile_list_row_servoing_kernel(
                 )
 
         def open_steer(hf, c0, width, numbers):
-            banks = [bank_tile(n, [P, n_tiles // len(numbers), width]) for n in numbers]
+            banks = [bank_tile(number, [P, n_tiles // len(numbers), width]) for number in numbers]
             steer_pass(0, banks, hf, c0)
             return banks
 
@@ -326,20 +314,19 @@ def tile_list_row_servoing_kernel(
                     result,
                 )
 
-        for c0 in range(0, BANK, PIECE):
-            for n0 in range(0, n_tiles, 2):
-                make_first_gate(c0, n0)
-        make_gate(1, 0)
-        make_gate(1, 1)
-        make_gate(1, 2)
+        for piece in range(BANK // PIECE):
+            for pair in range(n_tiles // 2):
+                make_gate(2 * piece + pair, 0, piece * PIECE, PIECE, 2 * pair)
+        for nt in range(n_tiles - 1):
+            make_gate(n_tiles + nt, 1, 0, BANK, nt)
         groups = [(hf, b) for hf in range(HALVES) for b in range(h_passes)]
         a_sq = {
             g: ring.tile([P, PACK, BANK], F32, name="total", bufs=len(groups), align_bytes=64) for g in groups
         }
         sums = dict(a_sq)
         square_on_vector(0, 0, 0)
-        make_gate(1, 3)
-        nc.scalar.activation(warm[:, 1:2], gate[1][:, 3, 0:1], ACT.Sqrt)
+        make_gate(0, 1, 0, BANK, n_tiles - 1)
+        nc.scalar.activation(warm[:, 1:2], gate[1][:, n_tiles - 1, 0:1], ACT.Sqrt)
         for t in range(1, EARLY_RUN):
             square_on_vector(0, 0, t)
         for t in range(EARLY_RUN):
@@ -362,7 +349,7 @@ def tile_list_row_servoing_kernel(
         for t in range(PACK):
             square_on_scalar(1, 1, t)
             add_terms(1, 1, t)
-        first_half = open_steer(0, 0, BANK, (7, 1, 2, 3))
+        first_half = open_steer(0, 0, BANK, ERROR_BANKS[0:PACK])
         for b in range(h_passes):
             magnitude(1, b, *TAIL[0][:2])
         close_steer(first_half, 0, 0, BANK)

@@ -29,7 +29,7 @@ GATES_AHEAD = PSUM_BANKS - 1
 ERROR_BANKS = (GATES_AHEAD,) + tuple(range(1, GATES_AHEAD)) + (0,)
 EARLY_RUN = 3
 LATE_RUN = 2
-ON_GPSIMD = {(0, 0, 0): BANK, (0, 0, 1): BANK // 2, (1, 0, 0): BANK // 2}
+ON_GPSIMD = {(0, 0, 0): BANK, (0, 0, 1): BANK // 4, (1, 0, 0): BANK // 2}
 TAIL = ((0, 256, ERROR_BANKS[4:6]), (256, 128, ERROR_BANKS[6:7]), (384, 128, (ERROR_BANKS[7], ERROR_BANKS[0])))
 
 

@@ -90,10 +90,10 @@ def tile_list_row_servoing_kernel(
         nc.sync.dma_start(
             tab_scale_win[2:P:4, :].bitcast(I32), tab_scales.rearrange("a q t -> q a t").bitcast(I32)
         )
-        for q in QUADRANTS:
+        for r in range(4):
             nc.sync.dma_start(
-                w1_scale_raw[32 * q : 32 * q + 4].bitcast(I32),
-                w1_scales[:, 4 * q : 4 * q + 4, :].rearrange("a r c -> r a c").bitcast(I32),
+                w1_scale_raw[r:P:32].bitcast(I32),
+                w1_scales[:, r:16:4, :].rearrange("a q c -> q a c").bitcast(I32),
             )
         nc.sync.dma_start(w2_raw[1][:], w2_rows[:, :, PASS : 2 * PASS])
 
@@ -326,7 +326,8 @@ def tile_list_row_servoing_kernel(
         sums = dict(a_sq)
         square_on_vector(0, 0, 0)
         make_gate(0, 1, 0, BANK, n_tiles - 1)
-        nc.scalar.activation(warm[:, 1:2], gate[1][:, n_tiles - 1, 0:1], ACT.Sqrt)
+        warm_root = held("w1_raw1", [P, 1], F32)
+        nc.scalar.activation(warm_root[:], warm[:, 0:1], ACT.Sqrt)
         for t in range(1, EARLY_RUN):
             square_on_vector(0, 0, t)
         for t in range(EARLY_RUN):

@@ -27,9 +27,7 @@ SPLIT = 3 * T // 8
 QUADRANTS = (0, 2, 1, 3)
 GATES_AHEAD = PSUM_BANKS - 1
 ERROR_BANKS = (GATES_AHEAD,) + tuple(range(1, GATES_AHEAD)) + (0,)
-EARLY_RUN = 3
-LATE_RUN = 2
-ON_GPSIMD = {(0, 0, 0): BANK, (0, 0, 1): BANK // 4, (1, 0, 0): BANK // 2}
+ON_GPSIMD = {(0, 0, 0): BANK, (0, 0, 1): BANK, (0, 1, 2): BANK, (0, 1, 3): BANK // 4}
 TAIL = ((0, 256, ERROR_BANKS[4:6]), (256, 128, ERROR_BANKS[6:7]), (384, 128, (ERROR_BANKS[7], ERROR_BANKS[0])))
 
 
@@ -45,7 +43,6 @@ def tile_list_row_servoing_kernel(
 
     with ExitStack() as ctx:
         keep = ctx.enter_context(tc.tile_pool(name="keep", bufs=1))
-        ring = ctx.enter_context(tc.tile_pool(name="ring", bufs=4))
         psum = ctx.enter_context(tc.psum_pool(name="psum", bufs=1))
 
         def held(name, shape, dtype):
@@ -61,7 +58,8 @@ def tile_list_row_servoing_kernel(
         tab_scale_win = held("tab_scale_win", [P, T], U8)
         tab2_scale_win = held("tab2_scale_win", [P, T], U8)
         w2_raw = [held("w2_raw%d" % b, [P, PACK, PASS], F32) for b in range(h_passes)]
-        w1_raw = [held("w1_raw%d" % a, [P, R], U16) for a in range(k_passes)]
+        gate_words = [held("gate_words%d" % a, [P, N], U16) for a in range(k_passes)]
+        err_raw = [held("err_raw%d" % b, [P, k_passes, PASS], U16) for b in range(h_passes)]
         w1_scale_raw = held("w1_scale_raw", [P, k_passes, R], U8)
         w1_plane = [held("w1_plane%d" % a, [P, H], U8) for a in range(k_passes)]
         w3_plane = held("w3_plane", [P, N], U8)
@@ -140,16 +138,19 @@ def tile_list_row_servoing_kernel(
                 v_plane[32 * q : 32 * q + 4, :].bitcast(I32),
                 v_scale_rows[32 * q + 2 : 32 * q + 32 : 4, :].bitcast(I32),
             )
-        nc.sync.dma_start(w1_raw[0][:, H:R].bitcast(I32), w1_words[0, :, 2 * H : 2 * R].bitcast(I32))
+        w1_thirds = w1_words.bitcast(I32).rearrange("a p (s c) -> s p a c", s=3)
+        nc.sync.dma_start(gate_words[0][:].bitcast(I32), w1_thirds[2, :, 0, :])
         nc.sync.dma_start(tab_win[1][:, SPLIT:T], last_pass[:, SPLIT:T])
 
         quantise_w2(1, (nc.scalar.copy, nc.vector.tensor_copy))
 
         b_sq = {}
+        b_groups = {}
         for b in range(h_passes):
             for hf in range(HALVES):
                 entries = slice(hf * BANK, (hf + 1) * BANK)
                 group = held("b_sq%d%d" % (b, hf), [P, PACK, BANK], F32)
+                b_groups[(hf, b)] = group
                 for t in range(PACK):
                     bank = bank_tile(PACK * hf + t, [P, BANK])
                     nc.tensor.matmul_mx(
@@ -168,8 +169,9 @@ def tile_list_row_servoing_kernel(
                 w1_plane[a][:].rearrange("p (b t c i) -> p b c t i", b=h_passes, t=PACK, i=16),
                 w1_scale_raw[:, a, 0:H].rearrange("p (b c i t) -> p b c t i", b=h_passes, t=PACK, i=16),
             )
-        nc.sync.dma_start(w1_raw[1][:].bitcast(I32), w1_words[1].bitcast(I32))
-        nc.sync.dma_start(w1_raw[0][:, 0:H].bitcast(I32), w1_words[0, :, 0 : 2 * H].bitcast(I32))
+        nc.sync.dma_start(err_raw[0][:].bitcast(I32), w1_thirds[0])
+        nc.sync.dma_start(gate_words[1][:].bitcast(I32), w1_thirds[2, :, 1, :])
+        nc.sync.dma_start(err_raw[1][:].bitcast(I32), w1_thirds[1])
         nc.sync.dma_start(w3_codes[:], w3_words.rearrange("a p c i -> p a (c i)").bitcast(I32))
         for q in QUADRANTS:
             nc.sync.dma_start(
@@ -178,8 +180,8 @@ def tile_list_row_servoing_kernel(
 
         v_codes = {}
 
-        def gather_words(a, hf, width):
-            codes = held("v_codes%d%d" % (a, hf), [P, BANK], U32)
+        def gather_words(a, hf, width, name):
+            codes = held(name, [P, BANK], U32)
             for c0 in range(0, BANK, width):
                 j0 = hf * BANK + c0
                 nc.vector.tensor_copy(
@@ -189,24 +191,28 @@ def tile_list_row_servoing_kernel(
             v_codes[(a, hf)] = codes
 
         for hf in range(HALVES):
-            gather_words(0, hf, BANK)
+            gather_words(0, hf, BANK, "v_codes0%d" % hf)
 
         for (hf, b, t), width in ON_GPSIMD.items():
             terms = b_sq[(hf, b, t)][:, 0:width]
             nc.vector.tensor_scalar_add(terms, terms, soft_sb[:, b, t : t + 1])
 
-        gather_words(1, 0, PIECE)
-        gather_words(1, 1, BANK)
+        err_words = {}
 
-        err_words = []
-        for b in range(h_passes):
-            words = held("err_words%d" % b, [P, k_passes, PASS], U16)
-            for a in range(k_passes):
-                nc.vector.tensor_copy(
-                    words[:, a, :].rearrange("p (t c i) -> p c t i", t=PACK, i=8),
-                    w1_raw[a][:, b * PASS : (b + 1) * PASS].rearrange("p (c i t) -> p c t i", t=PACK, i=8),
-                )
-            err_words.append(words)
+        def deal_words(b, a, copier):
+            words = held("err_words%d%d" % (b, a), [P, PASS], U16)
+            copier(
+                words[:].rearrange("p (t c i) -> p c t i", t=PACK, i=8),
+                err_raw[b][:, a, :].rearrange("p (c i t) -> p c t i", t=PACK, i=8),
+            )
+            err_words[(b, a)] = words
+
+        gather_words(1, 0, PIECE, "v_codes10")
+        deal_words(0, 0, nc.scalar.copy)
+        deal_words(0, 1, nc.vector.tensor_copy)
+        gather_words(1, 1, BANK, "err_raw0")
+        for a in range(k_passes):
+            deal_words(1, a, nc.vector.tensor_copy)
 
         def first_pass(sums_out, a, hf, c0, width, codes, plane, start, stop):
             j0 = a * S + hf * BANK + c0
@@ -226,65 +232,72 @@ def tile_list_row_servoing_kernel(
             bank = bank_tile(number, [P, per_bank, width])
             for a in range(k_passes):
                 for i in range(per_bank):
-                    cols = slice(H + P * (n0 + i), H + P * (n0 + i + 1))
+                    n1 = P * (n0 + i)
                     first_pass(
-                        bank[:, i, :], a, hf, c0, width, w1_raw[a][:, cols], w1_scale_raw[:, a, cols],
+                        bank[:, i, :], a, hf, c0, width, gate_words[a][:, n1 : n1 + P],
+                        w1_scale_raw[:, a, H + n1 : H + n1 + P],
                         a == 0 and i == 0, a == k_passes - 1 and i == per_bank - 1,
                     )
             nc.scalar.activation(gate[hf][:, n0 : n0 + per_bank, c0 : c0 + width], bank[:], ACT.Sigmoid)
 
-        def error_bank(hf, b, t):
-            bank = bank_tile(ERROR_BANKS[PACK * b + t], [P, BANK])
+        def error_bank(number, hf, b, t):
+            bank = bank_tile(number, [P, BANK])
             for a in range(k_passes):
                 first_pass(
-                    bank[:], a, hf, 0, BANK, err_words[b][:, a, t * P : (t + 1) * P],
+                    bank[:], a, hf, 0, BANK, err_words[(b, a)][:, t * P : (t + 1) * P],
                     w1_plane[a][:, b * PASS + t * P : b * PASS + (t + 1) * P],
                     a == 0, a == k_passes - 1,
                 )
             return bank
 
-        def square_on_scalar(hf, b, t):
-            nc.scalar.activation(a_sq[(hf, b)][:, t, :], error_bank(hf, b, t)[:], ACT.Square)
+        a_sq = {}
+        sums = {}
 
-        def square_on_vector(hf, b, t):
-            twice = error_bank(hf, b, t)[:].unsqueeze(2).to_broadcast([P, BANK, 2])
-            nc.vector.tensor_reduce(a_sq[(hf, b)][:, t, :], twice, mybir.AxisListType.X, ALU.mult)
+        def square_on_scalar(number, hf, b, t):
+            nc.scalar.activation(a_sq[(hf, b, t)], error_bank(number, hf, b, t)[:], ACT.Square)
 
-        def add_terms(hf, b, t):
-            squares = a_sq[(hf, b)][:, t, :]
-            total = sums[(hf, b)][:, t, :]
-            terms = b_sq[(hf, b, t)]
-            split = ON_GPSIMD.get((hf, b, t), 0)
-            if split > 0:
-                nc.gpsimd.tensor_tensor(total[:, 0:split], squares[:, 0:split], terms[:, 0:split], ALU.add)
-            if split < BANK:
-                nc.vector.scalar_tensor_tensor(
-                    total[:, split:BANK], squares[:, split:BANK], soft_sb[:, b, t : t + 1],
-                    terms[:, split:BANK], ALU.add, ALU.add,
-                )
+        def square_on_vector(number, hf, b, t):
+            twice = error_bank(number, hf, b, t)[:].unsqueeze(2).to_broadcast([P, BANK, 2])
+            nc.vector.tensor_reduce(a_sq[(hf, b, t)], twice, mybir.AxisListType.X, ALU.mult)
 
+        def add_on_gpsimd(total, squares, terms):
+            nc.gpsimd.tensor_tensor(total, squares, terms, ALU.add)
+
+        def add_on_vector(hf, b, t, c0, c1):
+            nc.vector.scalar_tensor_tensor(
+                sums[(hf, b)][:, t, c0:c1], a_sq[(hf, b, t)][:, c0:c1], soft_sb[:, b, t : t + 1],
+                b_sq[(hf, b, t)][:, c0:c1], ALU.add, ALU.add,
+            )
+
+        h_grouped = {}
         h_codes = {}
         h_plane = {}
 
-        def magnitude(hf, b, c0, width):
-            h_grouped = ring.tile([P, width, PACK], BF16, name="h_grouped", bufs=4, align_bytes=64)
+        def root(hf, b, c0, width):
+            grouped = held("h_grouped%d%d_%d" % (hf, b, c0), [P, width, PACK], BF16)
             nc.scalar.activation(
-                h_grouped[:].rearrange("p (c i) t -> p c t i", i=4),
+                grouped[:].rearrange("p (c i) t -> p c t i", i=4),
                 sums[(hf, b)][:, :, c0 : c0 + width].rearrange("p t (c i) -> p c t i", i=4),
                 ACT.Sqrt,
             )
+            h_grouped[(hf, b, c0)] = grouped
+
+        def quantise_h(hf, b, c0, width):
             codes = held("h_codes%d%d_%d" % (hf, b, c0), [P, width], U32)
             plane = held("h_plane%d%d_%d" % (hf, b, c0), [P, width], U8)
             nc.vector.quantize_mx(
                 out=codes[:].bitcast(FP8X4), scales=plane[:],
-                in_=h_grouped[:].rearrange("p j t -> p (j t)"),
+                in_=h_grouped[(hf, b, c0)][:].rearrange("p j t -> p (j t)"),
             )
             h_codes[(hf, b, c0)] = codes
             h_plane[(hf, b, c0)] = plane
 
-        def steer_pass(b, banks, hf, c0):
+        def steer_banks(width, numbers):
+            return [bank_tile(number, [P, n_tiles // len(numbers), width]) for number in numbers]
+
+        def steer_pass(b, banks, hf, c0, first, tiles=range(n_tiles)):
             per_bank = n_tiles // len(banks)
-            for nt in range(n_tiles):
+            for nt in tiles:
                 rows = slice(nt * P, (nt + 1) * P)
                 i = nt % per_bank
                 nc.tensor.matmul_mx(
@@ -293,69 +306,91 @@ def tile_list_row_servoing_kernel(
                     lhsT_scale=w3_plane[4 * b : P, rows],
                     rhs=h_codes[(hf, b, c0)][:].bitcast(FP8X4),
                     rhs_scale=h_plane[(hf, b, c0)][:],
-                    start=(b == 0 and i == 0), stop=(b == h_passes - 1 and i == per_bank - 1),
+                    start=(first and i == 0), stop=(not first and i == per_bank - 1),
                 )
 
-        def open_steer(hf, c0, width, numbers):
-            banks = [bank_tile(number, [P, n_tiles // len(numbers), width]) for number in numbers]
-            steer_pass(0, banks, hf, c0)
-            return banks
-
-        def close_steer(banks, hf, c0, width):
+        def gate_and_store(banks, hf, c0, width, stores):
             per_bank = n_tiles // len(banks)
-            steer_pass(1, banks, hf, c0)
+            j0 = hf * BANK + c0
+            stored = 0
             for k, bank in enumerate(banks):
-                n0 = k * per_bank
-                result = gate[hf][:, n0 : n0 + per_bank, c0 : c0 + width]
+                n1 = (k + 1) * per_bank
+                result = gate[hf][:, n1 - per_bank : n1, c0 : c0 + width]
                 nc.vector.tensor_tensor(result, bank[:], result, ALU.mult)
-                j0 = hf * BANK + c0
-                nc.sync.dma_start(
-                    out[n0 * P : (n0 + per_bank) * P, j0 : j0 + width].rearrange("(i p) j -> p i j", p=P),
-                    result,
-                )
+                if n1 in stores:
+                    nc.sync.dma_start(
+                        out[stored * P : n1 * P, j0 : j0 + width].rearrange("(i p) j -> p i j", p=P),
+                        gate[hf][:, stored:n1, c0 : c0 + width],
+                    )
+                    stored = n1
 
         for piece in range(BANK // PIECE):
             for pair in range(n_tiles // 2):
                 make_gate(2 * piece + pair, 0, piece * PIECE, PIECE, 2 * pair)
+        for hf in range(HALVES):
+            for b in range(h_passes):
+                sums[(hf, b)] = held("sums%d%d" % (hf, b), [P, PACK, BANK], F32)
+                for t in range(PACK):
+                    a_sq[(hf, b, t)] = sums[(hf, b)][:, t, :]
+        aside = held("aside", [P, 2, BANK], F32)
+        a_sq[(0, 1, 1)] = sums[(0, 1)][:, 2, :]
+        for t in (2, 3):
+            a_sq[(0, 1, t)] = aside[:, t - 2, :]
+
+        for t in range(2):
+            square_on_vector(ERROR_BANKS[t], 0, 0, t)
         for nt in range(n_tiles - 1):
             make_gate(n_tiles + nt, 1, 0, BANK, nt)
-        groups = [(hf, b) for hf in range(HALVES) for b in range(h_passes)]
-        a_sq = {
-            g: ring.tile([P, PACK, BANK], F32, name="total", bufs=len(groups), align_bytes=64) for g in groups
-        }
-        sums = dict(a_sq)
-        square_on_vector(0, 0, 0)
         make_gate(0, 1, 0, BANK, n_tiles - 1)
-        warm_root = held("w1_raw1", [P, 1], F32)
+        warm_root = held("gate_words1", [P, 1], F32)
         nc.scalar.activation(warm_root[:], warm[:, 0:1], ACT.Sqrt)
-        for t in range(1, EARLY_RUN):
-            square_on_vector(0, 0, t)
-        for t in range(EARLY_RUN):
-            add_terms(0, 0, t)
-        for t in range(EARLY_RUN, PACK):
-            square_on_scalar(0, 0, t)
-            add_terms(0, 0, t)
+        for t in (2, 3):
+            square_on_vector(ERROR_BANKS[t], 0, 0, t)
+        for t in range(2):
+            cols = slice(0, ON_GPSIMD[(0, 0, t)])
+            add_on_gpsimd(sums[(0, 0)][:, t, cols], a_sq[(0, 0, t)][:, cols], b_sq[(0, 0, t)][:, cols])
         for t in range(PACK):
-            square_on_scalar(0, 1, t)
-            add_terms(0, 1, t)
-        for t in range(LATE_RUN):
-            square_on_vector(1, 0, t)
-        magnitude(0, 0, 0, BANK)
-        sums[(1, 0)] = held("b_sq10", [P, PACK, BANK], F32)
-        magnitude(0, 1, 0, BANK)
-        for t in range(LATE_RUN, PACK):
-            square_on_scalar(1, 0, t)
+            if ON_GPSIMD.get((0, 0, t), 0) < BANK:
+                add_on_vector(0, 0, t, ON_GPSIMD.get((0, 0, t), 0), BANK)
         for t in range(PACK):
-            add_terms(1, 0, t)
+            square_on_scalar(ERROR_BANKS[PACK + t], 0, 1, t)
+        for t in range(2):
+            add_on_vector(0, 1, t, 0, BANK)
+        for t in range(2):
+            square_on_vector(ERROR_BANKS[t], 1, 0, t)
+        late = BANK + ON_GPSIMD[(0, 1, 3)]
+        add_on_gpsimd(
+            sums[(0, 1)][:, 2:4, :].rearrange("p t j -> p (t j)")[:, 0:late],
+            aside[:].rearrange("p t j -> p (t j)")[:, 0:late],
+            b_groups[(0, 1)][:, 2:4, :].rearrange("p t j -> p (t j)")[:, 0:late],
+        )
+        add_on_vector(0, 1, 3, ON_GPSIMD[(0, 1, 3)], BANK)
+        root(0, 0, 0, BANK)
+        quantise_h(0, 0, 0, BANK)
+        for t in (2, 3):
+            square_on_scalar(ERROR_BANKS[t], 1, 0, t)
+        root(0, 1, 0, BANK)
         for t in range(PACK):
-            square_on_scalar(1, 1, t)
-            add_terms(1, 1, t)
-        first_half = open_steer(0, 0, BANK, ERROR_BANKS[0:PACK])
+            add_on_vector(1, 0, t, 0, BANK)
+        quantise_h(0, 1, 0, BANK)
+        for t in range(PACK):
+            square_on_scalar(ERROR_BANKS[PACK + t], 1, 1, t)
+            add_on_vector(1, 1, t, 0, BANK)
+        first_half = steer_banks(BANK, ERROR_BANKS[0:PACK])
         for b in range(h_passes):
-            magnitude(1, b, *TAIL[0][:2])
-        close_steer(first_half, 0, 0, BANK)
+            steer_pass(b, first_half, 0, 0, b == 0)
+
+        def magnitudes(c0, width):
+            for b in range(h_passes):
+                root(1, b, c0, width)
+                quantise_h(1, b, c0, width)
+
+        magnitudes(*TAIL[0][:2])
+        gate_and_store(first_half, 0, 0, BANK, (2, 3, 4))
         for n, (c0, width, numbers) in enumerate(TAIL):
             if n + 1 < len(TAIL):
-                for b in range(h_passes):
-                    magnitude(1, b, *TAIL[n + 1][:2])
-            close_steer(open_steer(1, c0, width, numbers), 1, c0, width)
+                magnitudes(*TAIL[n + 1][:2])
+            banks = steer_banks(width, numbers)
+            for b in range(h_passes):
+                steer_pass(b, banks, 1, c0, b == 0)
+            gate_and_store(banks, 1, c0, width, (2, 4))

@@ -61,19 +61,15 @@ def tile_list_row_servoing_kernel(
         gate_words = [held("gate_words%d" % a, [P, N], U16) for a in range(k_passes)]
         err_raw = [held("err_raw%d" % b, [P, k_passes, PASS], U16) for b in range(h_passes)]
         w1_scale_raw = held("w1_scale_raw", [P, k_passes, R], U8)
-        w1_plane = [held("w1_plane%d" % a, [P, H], U8) for a in range(k_passes)]
+        w1_plane = held("w1_plane", [P, k_passes, H], U8)
         w3_plane = held("w3_plane", [P, N], U8)
         w3_codes = held("w3_codes", [P, h_passes, N], I32)
         soft_sb = held("soft_sb", [P, h_passes, PACK], F32)
         v_plane = held("v_plane", [P, k_passes * S], U8)
         v2_plane = held("v2_plane", [P, S], U8)
 
-        for window in (tab2_scale_win, tab_scale_win):
-            nc.vector.memset(window[:, 0 : T // 2].bitcast(I32), 0)
-            nc.gpsimd.memset(window[:, T // 2 : T].bitcast(I32), 0)
-        nc.vector.memset(w1_scale_raw[:].bitcast(I32), 0)
-        for plane in (v2_plane, v_plane, w3_plane):
-            nc.gpsimd.memset(plane[:].bitcast(I32), 0)
+        for cleared in (tab2_scale_win, tab_scale_win, w1_scale_raw, v2_plane, v_plane, w3_plane):
+            nc.gpsimd.memset(cleared[:].bitcast(I32), 0)
 
         warm = held("warm", [P, 2], F32)
         nc.gpsimd.memset(warm[:, 0:1], 0.0)
@@ -164,11 +160,10 @@ def tile_list_row_servoing_kernel(
                     nc.scalar.activation(group[:, t, :], bank[:], ACT.Square)
                     b_sq[(hf, b, t)] = group[:, t, :]
 
-        for a in range(k_passes):
-            nc.vector.tensor_copy(
-                w1_plane[a][:].rearrange("p (b t c i) -> p b c t i", b=h_passes, t=PACK, i=16),
-                w1_scale_raw[:, a, 0:H].rearrange("p (b c i t) -> p b c t i", b=h_passes, t=PACK, i=16),
-            )
+        nc.vector.tensor_copy(
+            w1_plane[:].rearrange("p a (b t m) -> p a b t m", b=h_passes, t=PACK),
+            w1_scale_raw[:, :, 0:H].rearrange("p a (b m t) -> p a b t m", b=h_passes, t=PACK),
+        )
         nc.sync.dma_start(err_raw[0][:].bitcast(I32), w1_thirds[0])
         nc.sync.dma_start(gate_words[1][:].bitcast(I32), w1_thirds[2, :, 1, :])
         nc.sync.dma_start(err_raw[1][:].bitcast(I32), w1_thirds[1])
@@ -188,14 +183,16 @@ def tile_list_row_servoing_kernel(
                     codes[:, c0 : c0 + width],
                     tab_win[a][:].bitcast(U32).indirect(idx[:, j0 // 16 : (j0 + width) // 16]),
                 )
-            v_codes[(a, hf)] = codes
+            v_codes[(a, hf)] = codes[:]
 
+        first_codes = held("v_codes0", [P, S], U32)
+        nc.vector.tensor_copy(first_codes[:], tab_win[0][:].bitcast(U32).indirect(idx[:]))
         for hf in range(HALVES):
-            gather_words(0, hf, BANK, "v_codes0%d" % hf)
+            v_codes[(0, hf)] = first_codes[:, hf * BANK : (hf + 1) * BANK]
 
         for (hf, b, t), width in ON_GPSIMD.items():
             terms = b_sq[(hf, b, t)][:, 0:width]
-            nc.vector.tensor_scalar_add(terms, terms, soft_sb[:, b, t : t + 1])
+            nc.gpsimd.tensor_scalar(terms, terms, soft_sb[:, b, t : t + 1], 1.0, ALU.add, ALU.mult)
 
         err_words = {}
 
@@ -205,14 +202,19 @@ def tile_list_row_servoing_kernel(
                 words[:].rearrange("p (t c i) -> p c t i", t=PACK, i=8),
                 err_raw[b][:, a, :].rearrange("p (c i t) -> p c t i", t=PACK, i=8),
             )
-            err_words[(b, a)] = words
+            err_words[(b, a)] = words[:]
 
         gather_words(1, 0, PIECE, "v_codes10")
         deal_words(0, 0, nc.scalar.copy)
         deal_words(0, 1, nc.vector.tensor_copy)
         gather_words(1, 1, BANK, "err_raw0")
+        late_words = held("err_words1", [P, k_passes, PASS], U16)
+        nc.vector.tensor_copy(
+            late_words[:].rearrange("p a (t c i) -> p a c t i", t=PACK, i=8),
+            err_raw[1][:].rearrange("p a (c i t) -> p a c t i", t=PACK, i=8),
+        )
         for a in range(k_passes):
-            deal_words(1, a, nc.vector.tensor_copy)
+            err_words[(1, a)] = late_words[:, a, :]
 
         def first_pass(sums_out, a, hf, c0, width, codes, plane, start, stop):
             j0 = a * S + hf * BANK + c0
@@ -245,7 +247,7 @@ def tile_list_row_servoing_kernel(
             for a in range(k_passes):
                 first_pass(
                     bank[:], a, hf, 0, BANK, err_words[(b, a)][:, t * P : (t + 1) * P],
-                    w1_plane[a][:, b * PASS + t * P : b * PASS + (t + 1) * P],
+                    w1_plane[:, a, b * PASS + t * P : b * PASS + (t + 1) * P],
                     a == 0, a == k_passes - 1,
                 )
             return bank

@@ -26,8 +26,12 @@ PIECE = BANK // 2
 SPLIT = 3 * T // 8
 QUADRANTS = (0, 2, 1, 3)
 GATES_AHEAD = PSUM_BANKS - 1
-ERROR_BANKS = (GATES_AHEAD,) + tuple(range(1, GATES_AHEAD)) + (0,)
-ON_GPSIMD = {(0, 0, 0): BANK, (0, 0, 1): BANK, (0, 1, 2): BANK, (0, 1, 3): BANK // 4}
+ERROR_BANKS = tuple(range(PSUM_BANKS))
+ON_GPSIMD = {(0, 0, 3): BANK, (0, 0, 0): BANK, (0, 0, 1): BANK // 2, (0, 1, 2): BANK, (0, 1, 3): BANK // 4}
+SOFT_AHEAD = {
+    (0, 0, 3): BANK, (0, 0, 0): BANK, (0, 0, 1): BANK // 2, (1, 0, 0): BANK, (1, 0, 1): BANK,
+    (0, 1, 2): BANK, (0, 1, 3): BANK // 4,
+}
 TAIL = ((0, 256, ERROR_BANKS[4:6]), (256, 128, ERROR_BANKS[6:7]), (384, 128, (ERROR_BANKS[7], ERROR_BANKS[0])))
 
 
@@ -190,7 +194,7 @@ def tile_list_row_servoing_kernel(
         for hf in range(HALVES):
             v_codes[(0, hf)] = first_codes[:, hf * BANK : (hf + 1) * BANK]
 
-        for (hf, b, t), width in ON_GPSIMD.items():
+        for (hf, b, t), width in SOFT_AHEAD.items():
             terms = b_sq[(hf, b, t)][:, 0:width]
             nc.gpsimd.tensor_scalar(terms, terms, soft_sb[:, b, t : t + 1], 1.0, ALU.add, ALU.mult)
 
@@ -331,30 +335,34 @@ def tile_list_row_servoing_kernel(
                 make_gate(2 * piece + pair, 0, piece * PIECE, PIECE, 2 * pair)
         for hf in range(HALVES):
             for b in range(h_passes):
-                sums[(hf, b)] = held("sums%d%d" % (hf, b), [P, PACK, BANK], F32)
+                name = "err_raw1" if (hf, b) == (0, 0) else "sums%d%d" % (hf, b)
+                sums[(hf, b)] = held(name, [P, PACK, BANK], F32)
                 for t in range(PACK):
                     a_sq[(hf, b, t)] = sums[(hf, b)][:, t, :]
         aside = held("aside", [P, 2, BANK], F32)
+        fed = held("fed", [P, BANK], F32)
+        a_sq[(0, 0, 3)] = fed[:]
         a_sq[(0, 1, 1)] = sums[(0, 1)][:, 2, :]
         for t in (2, 3):
             a_sq[(0, 1, t)] = aside[:, t - 2, :]
 
-        for t in range(2):
-            square_on_vector(ERROR_BANKS[t], 0, 0, t)
+        square_on_scalar(7, 0, 0, 3)
+        square_on_vector(0, 0, 0, 0)
         for nt in range(n_tiles - 1):
             make_gate(n_tiles + nt, 1, 0, BANK, nt)
-        make_gate(0, 1, 0, BANK, n_tiles - 1)
+        square_on_vector(1, 0, 0, 1)
+        make_gate(2, 1, 0, BANK, n_tiles - 1)
         warm_root = held("gate_words1", [P, 1], F32)
         nc.scalar.activation(warm_root[:], warm[:, 0:1], ACT.Sqrt)
-        for t in (2, 3):
-            square_on_vector(ERROR_BANKS[t], 0, 0, t)
-        for t in range(2):
+        square_on_vector(3, 0, 0, 2)
+        square_on_vector(4, 0, 1, 0)
+        for t in (3, 0, 1):
             cols = slice(0, ON_GPSIMD[(0, 0, t)])
             add_on_gpsimd(sums[(0, 0)][:, t, cols], a_sq[(0, 0, t)][:, cols], b_sq[(0, 0, t)][:, cols])
         for t in range(PACK):
             if ON_GPSIMD.get((0, 0, t), 0) < BANK:
                 add_on_vector(0, 0, t, ON_GPSIMD.get((0, 0, t), 0), BANK)
-        for t in range(PACK):
+        for t in range(1, PACK):
             square_on_scalar(ERROR_BANKS[PACK + t], 0, 1, t)
         for t in range(2):
             add_on_vector(0, 1, t, 0, BANK)
@@ -372,7 +380,9 @@ def tile_list_row_servoing_kernel(
         for t in (2, 3):
             square_on_scalar(ERROR_BANKS[t], 1, 0, t)
         root(0, 1, 0, BANK)
-        for t in range(PACK):
+        pair = sums[(1, 0)][:, 0:2, :]
+        nc.vector.tensor_tensor(pair, pair, b_groups[(1, 0)][:, 0:2, :], ALU.add)
+        for t in (2, 3):
             add_on_vector(1, 0, t, 0, BANK)
         quantise_h(0, 1, 0, BANK)
         for t in range(PACK):

@@ -27,12 +27,12 @@ SPLIT = 3 * T // 8
 QUADRANTS = (0, 2, 1, 3)
 GATES_AHEAD = PSUM_BANKS - 1
 ERROR_BANKS = tuple(range(PSUM_BANKS))
-ON_GPSIMD = {(0, 0, 3): BANK, (0, 0, 0): BANK, (0, 0, 1): BANK // 2, (0, 1, 2): BANK, (0, 1, 3): BANK // 4}
+ON_GPSIMD = {(0, 0, 3): BANK, (0, 0, 0): BANK, (0, 0, 1): BANK, (0, 1, 2): BANK, (0, 1, 3): BANK // 2}
 SOFT_AHEAD = {
-    (0, 0, 3): BANK, (0, 0, 0): BANK, (0, 0, 1): BANK // 2, (1, 0, 0): BANK, (1, 0, 1): BANK,
-    (0, 1, 2): BANK, (0, 1, 3): BANK // 4,
+    (0, 0, 3): BANK, (0, 0, 0): BANK, (0, 0, 1): BANK, (1, 0, 0): BANK, (1, 0, 1): BANK,
+    (0, 1, 2): BANK, (0, 1, 3): BANK // 2,
 }
-TAIL = ((0, 256, ERROR_BANKS[4:6]), (256, 128, ERROR_BANKS[6:7]), (384, 128, (ERROR_BANKS[7], ERROR_BANKS[0])))
+TAIL = ((0, 256, (6, 7)), (256, 128, (0,)), (384, 128, (3, 4)))
 
 
 def tile_list_row_servoing_kernel(
@@ -330,9 +330,6 @@ def tile_list_row_servoing_kernel(
                     )
                     stored = n1
 
-        for piece in range(BANK // PIECE):
-            for pair in range(n_tiles // 2):
-                make_gate(2 * piece + pair, 0, piece * PIECE, PIECE, 2 * pair)
         for hf in range(HALVES):
             for b in range(h_passes):
                 name = "err_raw1" if (hf, b) == (0, 0) else "sums%d%d" % (hf, b)
@@ -346,7 +343,10 @@ def tile_list_row_servoing_kernel(
         for t in (2, 3):
             a_sq[(0, 1, t)] = aside[:, t - 2, :]
 
-        square_on_scalar(7, 0, 0, 3)
+        for number in range(PACK):
+            if number == PACK - 1:
+                square_on_scalar(7, 0, 0, 3)
+            make_gate(number, 0, number // 2 * PIECE, PIECE, number % 2 * 2)
         square_on_vector(0, 0, 0, 0)
         for nt in range(n_tiles - 1):
             make_gate(n_tiles + nt, 1, 0, BANK, nt)
@@ -376,19 +376,19 @@ def tile_list_row_servoing_kernel(
         )
         add_on_vector(0, 1, 3, ON_GPSIMD[(0, 1, 3)], BANK)
         root(0, 0, 0, BANK)
-        quantise_h(0, 0, 0, BANK)
         for t in (2, 3):
             square_on_scalar(ERROR_BANKS[t], 1, 0, t)
         root(0, 1, 0, BANK)
+        add_on_vector(1, 0, 2, 0, BANK)
         pair = sums[(1, 0)][:, 0:2, :]
         nc.vector.tensor_tensor(pair, pair, b_groups[(1, 0)][:, 0:2, :], ALU.add)
-        for t in (2, 3):
-            add_on_vector(1, 0, t, 0, BANK)
+        quantise_h(0, 0, 0, BANK)
+        add_on_vector(1, 0, 3, 0, BANK)
         quantise_h(0, 1, 0, BANK)
         for t in range(PACK):
-            square_on_scalar(ERROR_BANKS[PACK + t], 1, 1, t)
+            square_on_scalar((6, 7, 0, 1)[t], 1, 1, t)
             add_on_vector(1, 1, t, 0, BANK)
-        first_half = steer_banks(BANK, ERROR_BANKS[0:PACK])
+        first_half = steer_banks(BANK, (4, 5, 2, 1))
         for b in range(h_passes):
             steer_pass(b, first_half, 0, 0, b == 0)
 

@@ -43,7 +43,6 @@ def tile_list_row_servoing_kernel(
     k_passes = K // PASS
     h_passes = H // PASS
     n_tiles = N // P
-    list_cols = BANK // 16
 
     with ExitStack() as ctx:
         keep = ctx.enter_context(tc.tile_pool(name="keep", bufs=1))
@@ -125,11 +124,8 @@ def tile_list_row_servoing_kernel(
 
         quantise_w2(0, (nc.scalar.copy,))
 
-        v2_codes = []
-        for hf in range(HALVES):
-            codes = held("v2_codes%d" % hf, [P, BANK], U16)
-            nc.vector.tensor_copy(codes[:], tab2_win[:].indirect(idx2[:, hf * list_cols : (hf + 1) * list_cols]))
-            v2_codes.append(codes)
+        v2_codes = held("v2_codes", [P, S], U16)
+        nc.vector.tensor_copy(v2_codes[:], tab2_win[:].indirect(idx2[:]))
 
         v_scale_rows = held("v_scale_rows", [P, S], U8)
         nc.vector.tensor_copy(v_scale_rows[:], tab_scale_win[:].indirect(idx[:]))
@@ -157,7 +153,7 @@ def tile_list_row_servoing_kernel(
                         out=bank[:],
                         lhsT=w2_codes[b][:, t * P : (t + 1) * P].bitcast(FP8X4),
                         lhsT_scale=w2_plane[b][:, t * P : (t + 1) * P],
-                        rhs=v2_codes[hf][:].bitcast(FP4X4),
+                        rhs=v2_codes[:, entries].bitcast(FP4X4),
                         rhs_scale=v2_plane[:, entries],
                         start=True, stop=True,
                     )
@@ -376,14 +372,14 @@ def tile_list_row_servoing_kernel(
         )
         add_on_vector(0, 1, 3, ON_GPSIMD[(0, 1, 3)], BANK)
         root(0, 0, 0, BANK)
+        quantise_h(0, 0, 0, BANK)
         for t in (2, 3):
             square_on_scalar(ERROR_BANKS[t], 1, 0, t)
         root(0, 1, 0, BANK)
-        add_on_vector(1, 0, 2, 0, BANK)
         pair = sums[(1, 0)][:, 0:2, :]
         nc.vector.tensor_tensor(pair, pair, b_groups[(1, 0)][:, 0:2, :], ALU.add)
-        quantise_h(0, 0, 0, BANK)
-        add_on_vector(1, 0, 3, 0, BANK)
+        for t in (2, 3):
+            add_on_vector(1, 0, t, 0, BANK)
         quantise_h(0, 1, 0, BANK)
         for t in range(PACK):
             square_on_scalar((6, 7, 0, 1)[t], 1, 1, t)

@@ -32,7 +32,7 @@ SOFT_AHEAD = {
     (0, 0, 3): BANK, (0, 0, 0): BANK, (0, 0, 1): BANK, (1, 0, 0): BANK, (1, 0, 1): BANK,
     (0, 1, 2): BANK, (0, 1, 3): BANK // 2,
 }
-TAIL = ((0, 256, (6, 7)), (256, 128, (0,)), (384, 128, (3, 4)))
+TAIL = ((0, 128, (6,)), (128, 128, (7,)), (256, 128, (0,)), (384, 128, (3, 4)))
 
 
 def tile_list_row_servoing_kernel(
@@ -291,8 +291,8 @@ def tile_list_row_servoing_kernel(
                 out=codes[:].bitcast(FP8X4), scales=plane[:],
                 in_=h_grouped[(hf, b, c0)][:].rearrange("p j t -> p (j t)"),
             )
-            h_codes[(hf, b, c0)] = codes
-            h_plane[(hf, b, c0)] = plane
+            h_codes[(hf, b, c0)] = codes[:]
+            h_plane[(hf, b, c0)] = plane[:]
 
         def steer_banks(width, numbers):
             return [bank_tile(number, [P, n_tiles // len(numbers), width]) for number in numbers]
@@ -306,8 +306,8 @@ def tile_list_row_servoing_kernel(
                     out=banks[nt // per_bank][:, i, :],
                     lhsT=w3_codes[:, b, rows].bitcast(FP8X4),
                     lhsT_scale=w3_plane[4 * b : P, rows],
-                    rhs=h_codes[(hf, b, c0)][:].bitcast(FP8X4),
-                    rhs_scale=h_plane[(hf, b, c0)][:],
+                    rhs=h_codes[(hf, b, c0)].bitcast(FP8X4),
+                    rhs_scale=h_plane[(hf, b, c0)],
                     start=(first and i == 0), stop=(not first and i == per_bank - 1),
                 )
 
@@ -389,9 +389,14 @@ def tile_list_row_servoing_kernel(
             steer_pass(b, first_half, 0, 0, b == 0)
 
         def magnitudes(c0, width):
-            for b in range(h_passes):
-                root(1, b, c0, width)
-                quantise_h(1, b, c0, width)
+            if c0 % PIECE == 0:
+                root(1, 0, c0, PIECE)
+                quantise_h(1, 0, c0, PIECE)
+                for tiles in (h_codes, h_plane):
+                    tiles[(1, 0, c0 + width)] = tiles[(1, 0, c0)][:, width:PIECE]
+                    tiles[(1, 0, c0)] = tiles[(1, 0, c0)][:, 0:width]
+            root(1, 1, c0, width)
+            quantise_h(1, 1, c0, width)
 
         magnitudes(*TAIL[0][:2])
         gate_and_store(first_half, 0, 0, BANK, (2, 3, 4))

from contextlib import ExitStack

import concourse.mybir as mybir

K, M, H, N, R, T, S = 1024, 512, 1024, 512, 1536, 4096, 1024
FLOPS = 2 * S * (K * R + M * H + H * N)

F32 = mybir.dt.float32
BF16 = mybir.dt.bfloat16
I32 = mybir.dt.int32
U32 = mybir.dt.uint32
U16 = mybir.dt.uint16
U8 = mybir.dt.uint8
FP8X4 = mybir.dt.float8_e4m3fn_x4
FP4X4 = mybir.dt.float4_e2m1fn_x4
ACT = mybir.ActivationFunctionType
ALU = mybir.AluOpType

P = 128
PACK = 4
PASS = P * PACK
BANK = 512
HALVES = S // BANK
PSUM_BANKS = 8
PIECE = BANK // 2
SPLIT = 3 * T // 8
QUADRANTS = (0, 2, 1, 3)
GATES_AHEAD = PSUM_BANKS - 1
ERROR_BANKS = tuple(range(PSUM_BANKS))
ON_GPSIMD = {(0, 0, 3): BANK, (0, 0, 0): BANK, (0, 0, 1): BANK, (0, 1, 2): BANK, (0, 1, 3): BANK // 2}
SOFT_AHEAD = {
    (0, 0, 3): BANK, (0, 0, 0): BANK, (0, 0, 1): BANK, (1, 0, 0): BANK, (1, 0, 1): BANK,
    (0, 1, 2): BANK, (0, 1, 3): BANK // 2,
}
TAIL = ((0, 128, (6,)), (128, 128, (7,)), (256, 128, (0,)), (384, 128, (3, 4)))


def tile_list_row_servoing_kernel(
    tc, tab_words, tab_scales, tab2_words, tab2_scales, offs, offs2,
    w1_words, w1_scales, w2, soft, w3_words, w3_scales, out,
):
    nc = tc.nc
    k_passes = K // PASS
    h_passes = H // PASS
    n_tiles = N // P

    with ExitStack() as ctx:
        keep = ctx.enter_context(tc.tile_pool(name="keep", bufs=1))
        psum = ctx.enter_context(tc.psum_pool(name="psum", bufs=1))

        def held(name, shape, dtype):
            return keep.tile(shape, dtype, name=name, align_bytes=256)

        def bank_tile(number, shape):
            return psum.tile(shape, F32, name="bank%d" % number)

        idx = held("idx", [P, S // 16], U16)
        idx2 = held("idx2", [P, S // 16], U16)
        tab_win = [held("tab_win%d" % a, [P, T], I32) for a in range(k_passes)]
        tab2_win = held("tab2_win", [P, T], U16)
        tab_scale_win = held("tab_scale_win", [P, T], U8)
        tab2_scale_win = held("tab2_scale_win", [P, T], U8)
        w2_raw = [held("w2_raw%d" % b, [P, PACK, PASS], F32) for b in range(h_passes)]
        gate_words = [held("gate_words%d" % a, [P, N], U16) for a in range(k_passes)]
        err_raw = [held("err_raw%d" % b, [P, k_passes, PASS], U16) for b in range(h_passes)]
        w1_scale_raw = held("w1_scale_raw", [P, k_passes, R], U8)
        w1_plane = held("w1_plane", [P, k_passes, H], U8)
        w3_plane = held("w3_plane", [P, N], U8)
        w3_codes = held("w3_codes", [P, h_passes, N], I32)
        soft_sb = held("soft_sb", [P, h_passes, PACK], F32)
        v_plane = held("v_plane", [P, k_passes * S], U8)
        v2_plane = held("v2_plane", [P, S], U8)

        for cleared in (tab2_scale_win, tab_scale_win, w1_scale_raw, v2_plane, v_plane, w3_plane):
            nc.gpsimd.memset(cleared[:].bitcast(I32), 0)

        warm = held("warm", [P, 2], F32)
        nc.gpsimd.memset(warm[:, 0:1], 0.0)
        nc.scalar.activation(warm[:, 1:2], warm[:, 0:1], ACT.Sigmoid)

        w2_rows = w2.rearrange("(p j) r -> p j r", j=PACK)
        nc.sync.dma_start(w2_raw[0][:], w2_rows[:, :, 0:PASS])
        nc.sync.dma_start(idx2[:], offs2)
        nc.sync.dma_start(tab2_scale_win[4:P:8, :].bitcast(I32), tab2_scales[0].bitcast(I32))
        nc.sync.dma_start(tab2_win[:].bitcast(I32), tab2_words[0].bitcast(I32))
        nc.sync.dma_start(idx[:], offs)
        nc.sync.dma_start(
            tab_scale_win[2:P:4, :].bitcast(I32), tab_scales.rearrange("a q t -> q a t").bitcast(I32)
        )
        for r in range(4):
            nc.sync.dma_start(
                w1_scale_raw[r:P:32].bitcast(I32),
                w1_scales[:, r:16:4, :].rearrange("a q c -> q a c").bitcast(I32),
            )
        nc.sync.dma_start(w2_raw[1][:], w2_rows[:, :, PASS : 2 * PASS])

        v2_scale_rows = held("v2_scale_rows", [P, S], U8)
        nc.vector.tensor_copy(v2_scale_rows[:], tab2_scale_win[:].indirect(idx2[:]))
        for r in range(4):
            nc.sync.dma_start(v2_plane[r:P:32, :].bitcast(I32), v2_scale_rows[8 * r + 4 : P : 32, :].bitcast(I32))
        nc.sync.dma_start(tab_win[0][:], tab_words[0].rearrange("p t i -> p (t i)").bitcast(I32))
        nc.sync.dma_start(soft_sb[:], soft.rearrange("(b p t) -> p b t", p=P, t=PACK))
        last_pass = tab_words[1].rearrange("p t i -> p (t i)").bitcast(I32)
        nc.sync.dma_start(tab_win[1][:, 0:SPLIT], last_pass[:, 0:SPLIT])

        w2_codes = []
        w2_plane = []

        def quantise_w2(b, copiers):
            grouped = held("w2_grouped%d" % b, [P, PACK, P, PACK], BF16)
            src = w2_raw[b][:].rearrange("p j (m t) -> p m j t", t=PACK)
            dst = grouped[:].rearrange("p t m j -> p m j t")
            for c, copier in enumerate(copiers):
                places = slice(c * P // len(copiers), (c + 1) * P // len(copiers))
                copier(dst[:, places], src[:, places])
            codes = held("w2_codes%d" % b, [P, PASS], U32)
            plane = held("w2_plane%d" % b, [P, PASS], U8)
            nc.vector.quantize_mx(
                out=codes[:].bitcast(FP8X4), scales=plane[:],
                in_=grouped[:].rearrange("p t m j -> p (t m j)"),
            )
            w2_codes.append(codes)
            w2_plane.append(plane)

        quantise_w2(0, (nc.scalar.copy,))

        v2_codes = held("v2_codes", [P, S], U16)
        nc.vector.tensor_copy(v2_codes[:], tab2_win[:].indirect(idx2[:]))

        v_scale_rows = held("v_scale_rows", [P, S], U8)
        nc.vector.tensor_copy(v_scale_rows[:], tab_scale_win[:].indirect(idx[:]))
        for q in QUADRANTS:
            nc.sync.dma_start(
                v_plane[32 * q : 32 * q + 4, :].bitcast(I32),
                v_scale_rows[32 * q + 2 : 32 * q + 32 : 4, :].bitcast(I32),
            )
        w1_thirds = w1_words.bitcast(I32).rearrange("a p (s c) -> s p a c", s=3)
        nc.sync.dma_start(gate_words[0][:].bitcast(I32), w1_thirds[2, :, 0, :])
        nc.sync.dma_start(tab_win[1][:, SPLIT:T], last_pass[:, SPLIT:T])

        quantise_w2(1, (nc.scalar.copy, nc.vector.tensor_copy))

        b_sq = {}
        b_groups = {}
        for b in range(h_passes):
            for hf in range(HALVES):
                entries = slice(hf * BANK, (hf + 1) * BANK)
                group = held("b_sq%d%d" % (b, hf), [P, PACK, BANK], F32)
                b_groups[(hf, b)] = group
                for t in range(PACK):
                    bank = bank_tile(PACK * hf + t, [P, BANK])
                    nc.tensor.matmul_mx(
                        out=bank[:],
                        lhsT=w2_codes[b][:, t * P : (t + 1) * P].bitcast(FP8X4),
                        lhsT_scale=w2_plane[b][:, t * P : (t + 1) * P],
                        rhs=v2_codes[:, entries].bitcast(FP4X4),
                        rhs_scale=v2_plane[:, entries],
                        start=True, stop=True,
                    )
                    nc.scalar.activation(group[:, t, :], bank[:], ACT.Square)
                    b_sq[(hf, b, t)] = group[:, t, :]

        nc.vector.tensor_copy(
            w1_plane[:].rearrange("p a (b t m) -> p a b t m", b=h_passes, t=PACK),
            w1_scale_raw[:, :, 0:H].rearrange("p a (b m t) -> p a b t m", b=h_passes, t=PACK),
        )
        nc.sync.dma_start(err_raw[0][:].bitcast(I32), w1_thirds[0])
        nc.sync.dma_start(gate_words[1][:].bitcast(I32), w1_thirds[2, :, 1, :])
        nc.sync.dma_start(err_raw[1][:].bitcast(I32), w1_thirds[1])
        nc.sync.dma_start(w3_codes[:], w3_words.rearrange("a p c i -> p a (c i)").bitcast(I32))
        for q in QUADRANTS:
            nc.sync.dma_start(
                w3_plane[32 * q : 32 * q + 8, :].bitcast(I32), w3_scales[:, 4 * q : 4 * q + 4, :].bitcast(I32)
            )

        v_codes = {}

        def gather_words(a, hf, width, name):
            codes = held(name, [P, BANK], U32)
            for c0 in range(0, BANK, width):
                j0 = hf * BANK + c0
                nc.vector.tensor_copy(
                    codes[:, c0 : c0 + width],
                    tab_win[a][:].bitcast(U32).indirect(idx[:, j0 // 16 : (j0 + width) // 16]),
                )
            v_codes[(a, hf)] = codes[:]

        first_codes = held("v_codes0", [P, S], U32)
        nc.vector.tensor_copy(first_codes[:], tab_win[0][:].bitcast(U32).indirect(idx[:]))
        for hf in range(HALVES):
            v_codes[(0, hf)] = first_codes[:, hf * BANK : (hf + 1) * BANK]

        for (hf, b, t), width in SOFT_AHEAD.items():
            terms = b_sq[(hf, b, t)][:, 0:width]
            nc.gpsimd.tensor_scalar(terms, terms, soft_sb[:, b, t : t + 1], 1.0, ALU.add, ALU.mult)

        err_words = {}

        def deal_words(b, a, copier):
            words = held("err_words%d%d" % (b, a), [P, PASS], U16)
            copier(
                words[:].rearrange("p (t c i) -> p c t i", t=PACK, i=8),
                err_raw[b][:, a, :].rearrange("p (c i t) -> p c t i", t=PACK, i=8),
            )
            err_words[(b, a)] = words[:]

        gather_words(1, 0, PIECE, "v_codes10")
        deal_words(0, 0, nc.scalar.copy)
        deal_words(0, 1, nc.vector.tensor_copy)
        gather_words(1, 1, BANK, "err_raw0")
        late_words = held("err_words1", [P, k_passes, PASS], U16)
        nc.vector.tensor_copy(
            late_words[:].rearrange("p a (t c i) -> p a c t i", t=PACK, i=8),
            err_raw[1][:].rearrange("p a (c i t) -> p a c t i", t=PACK, i=8),
        )
        for a in range(k_passes):
            err_words[(1, a)] = late_words[:, a, :]

        def first_pass(sums_out, a, hf, c0, width, codes, plane, start, stop):
            j0 = a * S + hf * BANK + c0
            nc.tensor.matmul_mx(
                out=sums_out,
                lhsT=codes.bitcast(FP4X4),
                lhsT_scale=plane,
                rhs=v_codes[(a, hf)][:, c0 : c0 + width].bitcast(FP8X4),
                rhs_scale=v_plane[:, j0 : j0 + width],
                start=start, stop=stop,
            )

        gate = [held("gate%d" % hf, [P, n_tiles, BANK], F32) for hf in range(HALVES)]

        def make_gate(number, hf, c0, width, n0):
            per_bank = BANK // width
            bank = bank_tile(number, [P, per_bank, width])
            for a in range(k_passes):
                for i in range(per_bank):
                    n1 = P * (n0 + i)
                    first_pass(
                        bank[:, i, :], a, hf, c0, width, gate_words[a][:, n1 : n1 + P],
                        w1_scale_raw[:, a, H + n1 : H + n1 + P],
                        a == 0 and i == 0, a == k_passes - 1 and i == per_bank - 1,
                    )
            nc.scalar.activation(gate[hf][:, n0 : n0 + per_bank, c0 : c0 + width], bank[:], ACT.Sigmoid)

        def error_bank(number, hf, b, t):
            bank = bank_tile(number, [P, BANK])
            for a in range(k_passes):
                first_pass(
                    bank[:], a, hf, 0, BANK, err_words[(b, a)][:, t * P : (t + 1) * P],
                    w1_plane[:, a, b * PASS + t * P : b * PASS + (t + 1) * P],
                    a == 0, a == k_passes - 1,
                )
            return bank

        a_sq = {}
        sums = {}

        def square_on_scalar(number, hf, b, t):
            nc.scalar.activation(a_sq[(hf, b, t)], error_bank(number, hf, b, t)[:], ACT.Square)

        def square_on_vector(number, hf, b, t):
            twice = error_bank(number, hf, b, t)[:].unsqueeze(2).to_broadcast([P, BANK, 2])
            nc.vector.tensor_reduce(a_sq[(hf, b, t)], twice, mybir.AxisListType.X, ALU.mult)

        def add_on_gpsimd(total, squares, terms):
            nc.gpsimd.tensor_tensor(total, squares, terms, ALU.add)

        def add_on_vector(hf, b, t, c0, c1):
            nc.vector.scalar_tensor_tensor(
                sums[(hf, b)][:, t, c0:c1], a_sq[(hf, b, t)][:, c0:c1], soft_sb[:, b, t : t + 1],
                b_sq[(hf, b, t)][:, c0:c1], ALU.add, ALU.add,
            )

        h_grouped = {}
        h_codes = {}
        h_plane = {}

        def root(hf, b, c0, width):
            grouped = held("h_grouped%d%d_%d" % (hf, b, c0), [P, width, PACK], BF16)
            nc.scalar.activation(
                grouped[:].rearrange("p (c i) t -> p c t i", i=4),
                sums[(hf, b)][:, :, c0 : c0 + width].rearrange("p t (c i) -> p c t i", i=4),
                ACT.Sqrt,
            )
            h_grouped[(hf, b, c0)] = grouped

        def quantise_h(hf, b, c0, width):
            codes = held("h_codes%d%d_%d" % (hf, b, c0), [P, width], U32)
            plane = held("h_plane%d%d_%d" % (hf, b, c0), [P, width], U8)
            nc.vector.quantize_mx(
                out=codes[:].bitcast(FP8X4), scales=plane[:],
                in_=h_grouped[(hf, b, c0)][:].rearrange("p j t -> p (j t)"),
            )
            h_codes[(hf, b, c0)] = codes[:]
            h_plane[(hf, b, c0)] = plane[:]

        def steer_banks(width, numbers):
            return [bank_tile(number, [P, n_tiles // len(numbers), width]) for number in numbers]

        def steer_pass(b, banks, hf, c0, first, tiles=range(n_tiles)):
            per_bank = n_tiles // len(banks)
            for nt in tiles:
                rows = slice(nt * P, (nt + 1) * P)
                i = nt % per_bank
                nc.tensor.matmul_mx(
                    out=banks[nt // per_bank][:, i, :],
                    lhsT=w3_codes[:, b, rows].bitcast(FP8X4),
                    lhsT_scale=w3_plane[4 * b : P, rows],
                    rhs=h_codes[(hf, b, c0)].bitcast(FP8X4),
                    rhs_scale=h_plane[(hf, b, c0)],
                    start=(first and i == 0), stop=(not first and i == per_bank - 1),
                )

        def gate_and_store(banks, hf, c0, width, stores):
            per_bank = n_tiles // len(banks)
            j0 = hf * BANK + c0
            stored = 0
            for k, bank in enumerate(banks):
                n1 = (k + 1) * per_bank
                result = gate[hf][:, n1 - per_bank : n1, c0 : c0 + width]
                nc.vector.tensor_tensor(result, bank[:], result, ALU.mult)
                if n1 in stores:
                    nc.sync.dma_start(
                        out[stored * P : n1 * P, j0 : j0 + width].rearrange("(i p) j -> p i j", p=P),
                        gate[hf][:, stored:n1, c0 : c0 + width],
                    )
                    stored = n1

        for hf in range(HALVES):
            for b in range(h_passes):
                name = "err_raw1" if (hf, b) == (0, 0) else "sums%d%d" % (hf, b)
                sums[(hf, b)] = held(name, [P, PACK, BANK], F32)
                for t in range(PACK):
                    a_sq[(hf, b, t)] = sums[(hf, b)][:, t, :]
        aside = held("aside", [P, 2, BANK], F32)
        fed = held("fed", [P, BANK], F32)
        a_sq[(0, 0, 3)] = fed[:]
        a_sq[(0, 1, 1)] = sums[(0, 1)][:, 2, :]
        for t in (2, 3):
            a_sq[(0, 1, t)] = aside[:, t - 2, :]

        for number in range(PACK):
            if number == PACK - 1:
                square_on_scalar(7, 0, 0, 3)
            make_gate(number, 0, number // 2 * PIECE, PIECE, number % 2 * 2)
        square_on_vector(0, 0, 0, 0)
        for nt in range(n_tiles - 1):
            make_gate(n_tiles + nt, 1, 0, BANK, nt)
        square_on_vector(1, 0, 0, 1)
        make_gate(2, 1, 0, BANK, n_tiles - 1)
        warm_root = held("gate_words1", [P, 1], F32)
        nc.scalar.activation(warm_root[:], warm[:, 0:1], ACT.Sqrt)
        square_on_vector(3, 0, 0, 2)
        square_on_vector(4, 0, 1, 0)
        for t in (3, 0, 1):
            cols = slice(0, ON_GPSIMD[(0, 0, t)])
            add_on_gpsimd(sums[(0, 0)][:, t, cols], a_sq[(0, 0, t)][:, cols], b_sq[(0, 0, t)][:, cols])
        for t in range(PACK):
            if ON_GPSIMD.get((0, 0, t), 0) < BANK:
                add_on_vector(0, 0, t, ON_GPSIMD.get((0, 0, t), 0), BANK)
        for t in range(1, PACK):
            square_on_scalar(ERROR_BANKS[PACK + t], 0, 1, t)
        for t in range(2):
            add_on_vector(0, 1, t, 0, BANK)
        for t in range(2):
            square_on_vector(ERROR_BANKS[t], 1, 0, t)
        late = BANK + ON_GPSIMD[(0, 1, 3)]
        add_on_gpsimd(
            sums[(0, 1)][:, 2:4, :].rearrange("p t j -> p (t j)")[:, 0:late],
            aside[:].rearrange("p t j -> p (t j)")[:, 0:late],
            b_groups[(0, 1)][:, 2:4, :].rearrange("p t j -> p (t j)")[:, 0:late],
        )
        add_on_vector(0, 1, 3, ON_GPSIMD[(0, 1, 3)], BANK)
        root(0, 0, 0, BANK)
        quantise_h(0, 0, 0, BANK)
        for t in (2, 3):
            square_on_scalar(ERROR_BANKS[t], 1, 0, t)
        root(0, 1, 0, BANK)
        pair = sums[(1, 0)][:, 0:2, :]
        nc.vector.tensor_tensor(pair, pair, b_groups[(1, 0)][:, 0:2, :], ALU.add)
        for t in (2, 3):
            add_on_vector(1, 0, t, 0, BANK)
        quantise_h(0, 1, 0, BANK)
        for t in range(PACK):
            square_on_scalar((6, 7, 0, 1)[t], 1, 1, t)
            add_on_vector(1, 1, t, 0, BANK)
        first_half = steer_banks(BANK, (4, 5, 2, 1))
        for b in range(h_passes):
            steer_pass(b, first_half, 0, 0, b == 0)

        def magnitudes(c0, width):
            if c0 % PIECE == 0:
                root(1, 0, c0, PIECE)
                quantise_h(1, 0, c0, PIECE)
                for tiles in (h_codes, h_plane):
                    tiles[(1, 0, c0 + width)] = tiles[(1, 0, c0)][:, width:PIECE]
                    tiles[(1, 0, c0)] = tiles[(1, 0, c0)][:, 0:width]
            root(1, 1, c0, width)
            quantise_h(1, 1, c0, width)

        magnitudes(*TAIL[0][:2])
        gate_and_store(first_half, 0, 0, BANK, (2, 3, 4))
        for n, (c0, width, numbers) in enumerate(TAIL):
            if n + 1 < len(TAIL):
                magnitudes(*TAIL[n + 1][:2])
            banks = steer_banks(width, numbers)
            for b in range(h_passes):
                steer_pass(b, banks, 1, c0, b == 0)
            gate_and_store(banks, 1, c0, width, (2, 4))
